import numpy as np, ml_dtypes
CORES = [40,41,42,43,44,45,46,47]
N = 8
import mx_ref
BF = ml_dtypes.bfloat16
def gentries(a):
    return np.ascontiguousarray(a.reshape(8, 16, -1).transpose(0, 2, 1)).reshape(8, -1)
def gtable(e):
    e = np.asarray(e); return np.ascontiguousarray(e.reshape(8, -1, 16).transpose(0, 2, 1)).reshape(128, -1).astype(np.int32)
def gcols(t, e):
    v = np.concatenate([t.reshape(8, 16, -1, 4), np.zeros((8, 16, 1, 4), BF)], axis=2)
    return np.ascontiguousarray(np.stack([v[g][:, e[g]] for g in range(8)])).reshape(128, -1)
def tile(rs):
    return np.stack(rs, axis=2).reshape(128, -1).astype(BF)
def pick(q, e):
    c = np.concatenate([q[0].reshape(128, -1, 4), np.zeros((128, 1, 4), np.uint8)], axis=1); s = np.concatenate([q[1], np.ones((16, 1), np.uint8)], axis=1)
    return (np.ascontiguousarray(c[:, e].reshape(128, -1)), np.ascontiguousarray(s[:, e]))
def join(*qs):
    return (np.concatenate([q[0] for q in qs], axis=1), np.concatenate([q[1] for q in qs], axis=1))
def put(q, e, v):
    c, s = q[0].reshape(128, -1, 4).copy(), q[1].copy(); c[:, e] = v[0].reshape(128, -1, 4); s[:, e] = v[1]
    return (c.reshape(128, -1), s)
def pk(c, s):
    return (np.ascontiguousarray(c), mx_ref.live(s))
def emit(q):
    return q[0], q[1]
def packed(v, rng):
    q = [mx_ref.quantize(np.ascontiguousarray(v[r])) for r in range(N)]
    return np.stack([a for a, b in q]), np.stack([mx_ref.plane(b, rng) for a, b in q])
def values_of_codes():
    e, c = np.zeros((128, 128, 4), np.float32), np.zeros((128, 2, 4), np.uint8)
    e[np.arange(128), np.arange(128), 0] = 1
    c[:127, :, 0] = np.arange(256).reshape(2, 128).T[:127]
    return mx_ref.matmul(mx_ref.quantize(e.reshape(128, 512).astype(BF)), (c.reshape(128, 8), np.full((16, 2), 127, np.uint8))).T.reshape(-1).astype(np.float64)
CODE_VALUE, SCALE_VALUE = values_of_codes(), 2.0 ** (np.arange(256) - 127.0)
def decode(q):
    return (CODE_VALUE[q[0]].reshape(16, 8, -1, 4) * SCALE_VALUE[q[1]][:, None, :, None] + 0.0).reshape(128, -1).astype(np.float32)
def f(rng, *shape):
    return mx_ref.flush((rng.standard_normal(shape, dtype=np.float32) * np.exp2(rng.integers(-2, 3, shape[:-1] + (1,)))).astype(BF))
def wide(rng, *shape, cols=0):
    v = rng.standard_normal(shape, dtype=np.float32) * np.exp2(rng.integers(-12, 13, shape)).astype(np.float32)
    if cols: v *= np.repeat(np.exp2(rng.integers(-cols, cols + 1, shape[:-2] + (1, shape[-1] // 4))) * (rng.random(shape[:-2] + (1, shape[-1] // 4)) > 0.0625), 4, axis=-1).astype(np.float32)
    return mx_ref.flush(v.astype(BF))
C, HALF = 320, 160
STEP = [1, 2, 4]
def big(v):
    v = v.astype(np.float32)
    v[np.abs(v) < np.float32(2.0 ** -16)] = 0
    return v.astype(BF)
def numbers_of(rng):
    return {"x": big(f(rng, N, 128, 4 * C)), "u": np.array(f(rng, N, 128, 512)), "v": np.array(f(rng, N, 128, 512))}
def lists(rng):
    e = np.tile(np.arange(C), (N, 8, 1))
    o = rng.permuted(e, axis=2)
    m = np.zeros((N, 8, C), np.int64)
    np.put_along_axis(m, o, o[:, :, np.arange(C) ^ 1], axis=2)
    return rng.permuted(e, axis=2), m
def stored(q, m):
    return {"gq": np.stack([gtable(q[r]) for r in range(N)]), "gm": np.stack([gtable(m[r]) for r in range(N)])}
def layers(rng):
    return big(f(rng, N, 128, 2048)).reshape(N, 8, 16, 4, 8, 16, 4)
def no_layers():
    return np.zeros((N, 8, 16, 4, 8, 16, 4), np.float32)
def weights(rng, w):
    c, p = packed(np.ascontiguousarray(w.astype(BF)).reshape(N, 128, 2048), rng)
    return {"wc": c, "ws": p}
def setup_inputs(rng):
    return {**numbers_of(rng), **stored(*lists(rng)), **weights(rng, layers(rng))}
def setup_inputs_ties(rng):
    d = numbers_of(rng)
    o = rng.permutation(N)
    q, m = lists(rng)
    k = rng.integers(-1, 2, (N, 8, C)).astype(np.float32)
    k[o[0], rng.permutation(8)[:4]] = 0
    k[o[1]] = np.where(rng.permutation(8) < 4, 1, -1)[:, None]
    k[o[3]] = np.where(np.arange(C) < HALF, 1, -3)
    for g in range(8):
        a, b, p = rng.permutation(HALF), HALF + rng.permutation(HALF), rng.permutation(HALF)
        q[o[3], g] = np.concatenate([a, b] if g == 0 else [b, a])
        m[o[3], g, :HALF] = HALF + p
        m[o[3], g, HALF + p] = np.arange(HALF)
    x = d["x"].reshape(N, 8, 16, C, 4)
    x[:, :, 0] = 0
    x[:, :, 0, :, 0] = k.astype(BF)
    u = d["u"].reshape(N, 128, 128, 4)
    u[:, :, ::16] = 0
    for h in range(0, 128, 16): u[:, h, h, 0] = 1
    w = layers(rng)
    w[:, :, :, :, :, 0] = 0
    return {"x": x.reshape(N, 128, 4 * C), "u": u.reshape(N, 128, 512), "v": d["v"], **stored(q, m), **weights(rng, w)}
def setup_inputs_near(rng):
    d = numbers_of(rng)
    o = rng.permutation(N) % 2
    k = np.where(o == 0, 2.0 ** -30, 1.0)
    x = np.zeros((N, 8, 16, C, 4))
    s = rng.integers(-1, 2, (N, 8, C)) * k[:, None, None]
    x[:, :, 0, :, 0] = 1.125 * s
    x[:, :, 1, :, 0] = -1.25 * s
    x[:, :, 7, :, 0] = 2.0 ** -30
    x[:, :, 8, :, 0] = 2.0 ** -30
    for r in range(N):
        at = [0, C - 1, int(rng.integers(C)), int(rng.integers(C))]
        for g, j in zip(rng.permutation(8)[:4], at): x[r, g, 0, j, 0] = 2.0 ** 30 * rng.choice([-1.0, 1.0])
    u = d["u"].reshape(N, 128, 128, 4)
    u[:, :, ::16] = 0
    for h in range(0, 128, 16):
        u[:, h, h, 0] = (1.125 * k).astype(np.float32).astype(BF)
        u[:, h + 1, h, 0] = k.astype(np.float32).astype(BF)
        u[:, h + 9, h, 0] = 2.0 ** -30
    w = no_layers()
    for g in range(8):
        w[:, g, 8, 0, g, 8, 0] = 32
        w[:, g, 1, 0, g, 9, 0] = np.where(o == 0, 2.0 ** -9, 2.0 ** -30)
    return {"x": x.astype(np.float32).reshape(N, 128, 4 * C).astype(BF), "u": u.reshape(N, 128, 512), "v": d["v"], **stored(*lists(rng)), **weights(rng, w)}
def setup_inputs_odd(rng):
    d = numbers_of(rng)
    x = (1.0 + (2 * rng.integers(0, 64, (N, 8, 16, C, 4)) + 1) * 2.0 ** -7) * np.exp2(-rng.integers(0, 7, (N, 8, 16, C, 4)).astype(np.float64)) * rng.choice([-1.0, 1.0], (N, 8, 16, C, 4))
    e = rng.choice([-1.0, 1.0], (N, 8, C)) * 2.0 ** -8
    n = rng.integers(0, 2, (N, 8, C))
    x[:, :, 8:] = 0
    x[:, :, 0, :, 0] = 1.96875 * 2.0 ** 8 * rng.choice([-1.0, 1.0], (N, 8, 1))
    x[:, :, 1, :, 0] = np.where(n == 0, 5.0, 7.0) * e
    x[:, :, 8, :, 0] = np.where(n == 0, -4.5, -7.5) * e
    x[:, :, 10, :, 0] = 1.125 * 2.0 ** -2
    u = d["u"].reshape(N, 128, 128, 4)
    u[:, :, ::16] = 0
    for h in range(0, 128, 16):
        u[:, h + 1, h, 0] = 1
        u[:, h + 8, h, 0] = 1
    w = no_layers()
    for g in range(8):
        w[:, g, 10, 0, g, 9, 0] = 1.75 * 2.0 ** 5
        for b in range(4): w[:, g, 10, b, g, 11:, 0] = rng.choice([1.125, 1.5, 2.0], (N, 5)) * 2.0 ** -9
    return {"x": x.astype(np.float32).reshape(N, 128, 4 * C).astype(BF), "u": u.reshape(N, 128, 512), "v": d["v"], **stored(*lists(rng)), **weights(rng, w)}
def setup_inputs_ends(rng):
    d = numbers_of(rng)
    o, e, h = rng.permutation(N) % 4, rng.permutation(N) % 4, rng.permutation(8)
    s = rng.choice([-1.0, 1.0], (N, 128, C, 4))
    s[o == 0] = -1
    s[o == 1] = rng.choice([-1.0, 1.0], (N, 1, C, 1))[o == 1]
    x = s * (0.955 + 0.02 * rng.random((N, 128, C, 4))) * 2.0 ** 30
    x[o == 3] = 2.0 ** -30
    size = np.where(o == 3, 2.0 ** -30, 2.0 ** 30)
    a = np.stack([rng.permutation(8) % 2 * 2.0 - 1.0 for r in range(N)]) * size[:, None]
    u = d["u"].reshape(N, 128, 128, 4)
    u[:, :, ::16] = a.astype(np.float32).astype(BF)[:, None, :, None]
    v = rng.choice([-1.0, 1.0], (N, 128, 512)) * np.where(o % 2 == 0, 2.0 ** 30, 2.0 ** -30)[:, None, None]
    q, m = lists(rng)
    c = np.arange(C)
    q[e == 0], m[e == 0] = c, C - 1 - c
    q[e == 1], m[e == 1] = C - 1 - c, c ^ 1
    q[e == 2], m[e == 2] = (c + 1) % C, (c + HALF) % C
    w = no_layers()
    i = np.arange(16)
    for r in range(N):
        for b in range(4):
            if o[r] < 3:
                for g in h[:3]: w[r, g, i, b, g, i, b] = -0.125
            w[r, h[4], i, b, h[3], i, b] = 2.0 ** 30 if o[r] == 3 else 2.0 ** -30
    return {"x": x.astype(np.float32).reshape(N, 128, 4 * C).astype(BF), "u": u.reshape(N, 128, 512), "v": v.astype(np.float32).astype(BF), **stored(q, m), **weights(rng, w)}
def setup_inputs_spread(rng):
    d = setup_inputs(rng)
    d["x"] = big(wide(rng, N, 128, 4 * C, cols=6))
    return d
def check_inputs(d):
    b = []
    for k in ("x", "u", "v"):
        a = np.abs(d[k].astype(np.float32))
        if not (np.isfinite(a).all() and ((a == 0) | (a >= 2.0 ** -30) & (a <= 2.0 ** 30)).all()): b.append("a value of " + k)
    none, least, most = [emit(mx_ref.quantize(np.full((128, 16), k, np.float32).astype(BF)))[1][0, 0] for k in (0.0, 2.0 ** -30, 2.0 ** 30)]
    c = np.arange(C)
    for r in range(N):
        if not (np.sort(gentries(d["gq"][r]), axis=1) == c).all(): b.append("gq: not each column once in a group")
        m = gentries(d["gm"][r])
        if not ((m >= 0) & (m < C)).all(): b.append("an entry of gm")
        elif not ((np.take_along_axis(m, m, axis=1) == c) & (m != c)).all(): b.append("gm: not pairs")
        if ((d["wc"][r] == 0x7F) | (d["wc"][r] == 0xFF)).any(): b.append("wc: a code that is no number")
        s = mx_ref.live(d["ws"][r])
        if ((s != none) & ((s < least) | (s > most))).any(): b.append("ws: a scale out of range")
        if (((d["wc"][r].reshape(16, 8, 512, 4) & 0x7F) != 0) & (s == none)[:, None, :, None]).any(): b.append("wc: a code other than zero under the scale of zeros")
    return b
def exchange(s, m):
    bit = np.roll(s[::16] > 0, 1, axis=0)
    return np.where(np.take_along_axis(bit, np.minimum(m, np.arange(C)), axis=1), m, np.arange(C))
def reference(x, u, v, gq, gm, wc, ws):
    qu = [mx_ref.quantize(u[r]) for r in range(N)]
    lay = [pk(wc[r], ws[r]) for r in range(N)]
    kept, pair = [gentries(gq[r]) for r in range(N)], [gentries(gm[r]) for r in range(N)]
    now = [x[r] for r in range(N)]
    for step in STEP:
        mid, back, sent = [], [], []
        for r in range(N):
            q, m = kept[r], pair[r]
            a, b = np.zeros((9, C), np.int64), np.zeros((9, C), np.int64)
            go = exchange(mx_ref.matmul(qu[r], mx_ref.quantize(now[r])), m)
            a[0] = np.arange(C)
            for g in range(8): a[g + 1] = q[g][go[g][a[g]]]
            t = ((now[r].astype(np.float32) + gcols(now[r], a[1:]).astype(np.float32)) * np.float32(0.5)).astype(BF)
            qt = mx_ref.quantize(t)
            go = exchange(mx_ref.matmul(qu[r], qt), m)
            inv = np.argsort(q, axis=1)
            b[8] = a[8]
            for g in range(7, -1, -1): b[g] = go[g][inv[g][b[g + 1]]]
            sent.append(mx_ref.quantize(tile([mx_ref.matmul(pick(lay[r], np.arange(128 * k, 128 * k + 128)), qt) * np.float32(0.03125) for k in range(4)])))
            miss = np.take_along_axis(a[:8] != b[:8], np.minimum(m, np.arange(C)), axis=1)
            kept[r] = np.where(miss, np.take_along_axis(q, m, axis=1), q)
            mid.append(t)
            back.append(b[:8])
        now = [(mid[r].astype(np.float32) + gcols(decode(sent[r ^ step]).astype(BF), back[r]).astype(np.float32)).astype(BF) for r in range(N)]
    y, qo = np.zeros((N, 128, C), np.float32), np.zeros((N, 8, C), np.float32)
    oc, osc = np.zeros((N, 128, 4 * C), np.uint8), np.zeros((N, 16, C), np.uint8)
    for r in range(N):
        q = mx_ref.quantize(now[r])
        y[r] = mx_ref.matmul(mx_ref.quantize(v[r]), q)
        qo[r] = kept[r]
        oc[r], osc[r] = emit(q)
    return {"y": y, "qo": qo, "oc": oc, "osc": osc}

@@ -1,0 +1,469 @@
+from concourse.mybir import dt, AluOpType as A, ActivationFunctionType as F
+
+C = 320
+ROUNDS = (1, 2, 4)
+HALVES = ((0, 160), (160, 320))
+EPS = 2.0 ** -93
+
+SCRATCH = {}
+
+
+def _buf(dtype, **widths):
+    for k, n in widths.items():
+        SCRATCH[k] = ("sbuf", [128, n], dtype)
+
+
+_buf("bfloat16", xt=1280, xn0=1280, xn1=1280, xn2=1280, xp=1280, xi=960, vt=1280, ht=1280, dp=1280, ut=512, vv=512, et=2048, ones=512,
+     iot=320, hs=80, hc=320, tw=48, z01=640, ys=640, yv=640, qr=320, qmr=320, qir=320, mr=320, mqr=320, d0f=640, d1f=640, d0b=640, d1b=640,
+     tf=320, tb=320, w=640, sg=320, frf=1440, frb=1440, t1=352, t1p=352, tt=320, rr=160, rr8=160, mm=320, tm=320,
+     ac=32, at=32, a2=32, bc=32, bt=32, md=32, cu0=32, cu1=32, cut=32)
+_buf("float32", sm=120, ie=20, col=16, iwc=20, vf=10, qf=20, mf=20, qmw=20, qiw=20, mqw=20, wm=320, qout=320, yt=320)
+_buf("int32", icol=4, offi=8, gqs=20, gms=20)
+_buf("uint16", offu=8, k16=20, qo16=20, mo16=20, qio=20, kof=20, kob=20, lof=20, hif=20, tif=20, hib=20, tib=20, fl=22, sl=10, slb=10, ll=20, llb=20, xo=20, xob=20, moff=32, ktf=20, ktb=20)
+for _n, _w in (("uq", 128), ("us", 128), ("xq", 320), ("vq", 320), ("vvq", 128), ("eq", 512), ("wq", 512), ("hq", 960), ("rq", 960)):
+    SCRATCH[_n + "c"] = ("sbuf", [128, _w], "float8_e4m3fn_x4")
+    SCRATCH[_n + "s"] = ("sbuf", [128, _w], "uint8")
+for _b in range(8):
+    SCRATCH["ps%d" % _b] = ("psum", [128, 512], "float32")
+
+NDMA = 20
+SEMAPHORES = ["qv", "qs", "qt", "qg", "lsem"] + ["d%d" % i for i in range(NDMA)] + ["ar%d_%d" % (r, h) for r in range(3) for h in range(2)]
+
+PLACE = {"tw1": ("tw", 0, 16), "tw2": ("tw", 32, 16)}
+PLACE.update({n: ("col", i, 1) for i, n in enumerate(("kf", "mo", "hh", "p31f", "s1", "b1", "s2", "b2", "gg", "sgo"))})
+PLACE.update({n: ("icol", i, 1) for i, n in enumerate(("pi", "ki", "si", "p31"))})
+PLACE.update({n: ("hs", 16 * i, 16) for i, n in enumerate(("j16", "df", "ha", "hb", "hc16"))})
+PLACE.update({n: ("sm", 20 * i, 20) for i, n in enumerate(("kw", "low", "hiw", "tiw", "kta", "ktc"))})
+
+
+def R(name, c0=0, c1=None, st=1, p0=0, p1=128):
+    if name in PLACE:
+        name, at, n = PLACE[name]
+        return (name, at + c0, at + (n if c1 is None else c1), st, p0, p1)
+    return (name, c0, SCRATCH[name][1][1] if c1 is None else c1, st, p0, p1)
+
+
+def rank_program(g, core, T, topo):
+    rank = T.rank_of(core)
+    if rank is None:
+        return
+    queue = {"v": g.vector, "s": g.scalar, "t": g.tensor, "g": g, "y": g.sync}
+    count = {"qv": 0, "qs": 0, "qt": 0, "qg": 0}
+    known = {k: {} for k in queue}
+    clock = {}
+    writes, reads = {}, {}
+    pending = {}
+    state = {"bank": 0, "dma": 0}
+
+    def ap(r):
+        name, c0, c1, st, p0, p1 = r
+        return T[name][p0:p1, c0:c1:st] if st > 1 else T[name][p0:p1, c0:c1]
+
+    def hit(a, b):
+        if a[4] >= b[5] or b[4] >= a[5] or a[1] >= b[2] or b[1] >= a[2]:
+            return False
+        s = min(a[3], b[3])
+        return not (s > 1 and max(a[3], b[3]) % s == 0 and (a[1] - b[1]) % s)
+
+    def inside(a, b):
+        return a[4] >= b[4] and a[5] <= b[5] and a[1] >= b[1] and a[2] <= b[2] and (b[3] == 1 or (a[3] == b[3] and (a[1] - b[1]) % a[3] == 0))
+
+    def settle(q, events):
+        for sem, val in sorted(events, key=lambda e: (-len(clock[e]), e[0], -e[1])):
+            if known[q].get(sem, 0) < val:
+                queue[q].wait_ge(T.sem[sem], val)
+                for s, v in clock[(sem, val)].items():
+                    known[q][s] = max(known[q].get(s, 0), v)
+                known[q][sem] = val
+
+    def order(q, outs, ins):
+        ev = set()
+        for r in ins:
+            ev |= {e for w, e in writes.get(r[0], []) if hit(r, w)}
+        for r in outs:
+            ev |= {e for w, e in writes.get(r[0], []) if hit(r, w)}
+            ev |= {e for w, e in reads.get(r[0], []) if hit(r, w) and e[0] != "q" + q}
+        settle(q, ev)
+
+    def note(outs, ins, ev):
+        for r in outs:
+            for book in (writes, reads):
+                book[r[0]] = [(w, e) for w, e in book.get(r[0], []) if not inside(w, r)]
+            writes[r[0]].append((r, ev))
+        for r in ins:
+            reads.setdefault(r[0], []).append((r, ev))
+
+    def op(q, outs, ins, fn):
+        order(q, outs, ins)
+        sem = "q" + q
+        clk = dict(known[q])
+        fn().then_inc(T.sem[sem], 1)
+        count[sem] += 1
+        clk[sem] = count[sem]
+        clock[(sem, count[sem])] = clk
+        note(outs, ins, (sem, count[sem]))
+
+    def dma(q, outs, ins, dst, src):
+        order(q, outs, ins)
+        sem = "d%d" % state["dma"]
+        state["dma"] += 1
+        clock[(sem, 16)] = dict(known[q])
+        queue[q].dma_start(dst, src).then_inc(T.sem[sem], 16)
+        pending[sem] = 16
+        note(outs, ins, (sem, 16))
+
+    def copy(out, src):
+        op("v", [out], [src], lambda: g.vector.tensor_copy(ap(out), ap(src)))
+
+    def pick(q, out, win, off):
+        if q == "v":
+            op(q, [out], [win, off], lambda: g.vector.tensor_copy(ap(out), ap(win).indirect(ap(off))))
+        else:
+            op(q, [out], [win, off], lambda: g.scalar.activation(ap(out), ap(win).indirect(ap(off)), F.Copy))
+
+    def pick_tt(out, win, off, other, alu):
+        op("v", [out], [win, off, other], lambda: g.vector.tensor_tensor(ap(out), ap(win).indirect(ap(off)), ap(other), alu))
+
+    def ts(out, src, s1, op0, s2=None, op1=None):
+        col = [s for s in (s1, s2) if isinstance(s, tuple)]
+        a1 = ap(s1) if isinstance(s1, tuple) else s1
+        a2 = ap(s2) if isinstance(s2, tuple) else s2
+        if op1 is None:
+            op("v", [out], [src] + col, lambda: g.vector.tensor_scalar(ap(out), ap(src), a1, None, op0))
+        else:
+            op("v", [out], [src] + col, lambda: g.vector.tensor_scalar(ap(out), ap(src), a1, a2, op0, op1))
+
+    def tt(out, a, b, alu):
+        op("v", [out], [a, b], lambda: g.vector.tensor_tensor(ap(out), ap(a), ap(b), alu))
+
+    def fill(out, val):
+        op("v", [out], [], lambda: g.vector.memset(ap(out), val))
+
+    def iota(out, pattern, base, cm):
+        op("g", [out], [], lambda: g.iota(ap(out), pattern, base, cm, allow_small_or_imprecise_dtypes=True))
+
+    def turn(out, src):
+        op("v", [out], [src], lambda: g.vector.transpose(ap(out), ap(src)))
+
+    def scan(out, d0, d1, op0, op1):
+        op("v", [out], [d0, d1], lambda: g.vector.tensor_tensor_scan(ap(out), ap(d0), ap(d1), 0.0, op0, op1))
+
+    def quant(name, src, c0, c1):
+        o, s = R(name + "c", c0, c1), R(name + "s", c0, c1)
+        op("v", [o, s], [src], lambda: g.vector.quantize_mx(ap(o), ap(s), ap(src)))
+
+    def mx(bank, n, wname, w0, mname, m0):
+        w, ws, m, ms = R(wname + "c", w0, w0 + 128), R(wname + "s", w0, w0 + 128), R(mname + "c", m0, m0 + n), R(mname + "s", m0, m0 + n)
+        o = R("ps%d" % bank, 0, n)
+        op("t", [R("ps%d" % bank)], [w, ws, m, ms], lambda: g.tensor.matmul_mx(ap(o), ap(w), ap(ws), ap(m), ap(ms), True, True))
+
+    def act(out, src, func, scale=1.0, bias=0.0):
+        op("s", [out], [src], lambda: g.scalar.activation(ap(out), ap(src), func, bias=bias, scale=scale))
+
+    def unrow(dst, src):
+        scan(R("wm"), R("hc"), R(src), A.add, A.max)
+        ts(R(dst), R("wm", 15, 320, 16), one("hh"), A.subtract)
+
+    waiting = []
+
+    def spare():
+        if waiting:
+            waiting.pop(0)()
+
+    dma("y", [R("gqs")], [], ap(R("gqs")), T.gq[:, :])
+    dma("y", [R("gms")], [], ap(R("gms")), T.gm[:, :])
+    dma("y", [R("xt")], [], ap(R("xt")), T.x[:, :])
+    dma("s", [R("ut")], [], ap(R("ut")), T.u[:, :])
+    order("y", [], [R("xt")])
+    dma("y", [R("wqc")], [], T.wqc[:, :].bitcast(dt.uint8), T.wc[:, :])
+    dma("y", [R("wqs")], [], T.wqs[:, :], T.ws[:, :])
+    dma("y", [R("vv")], [], ap(R("vv")), T.v[:, :])
+
+    def one(n, p0=0, p1=128):
+        return R(n, 0, 1, 1, p0, p1)
+
+    def bits(out, s1, op0, s2=None, op1=None):
+        if op1 is None:
+            op("v", [one(out)], [one("pi")], lambda: g.vector.tensor_scalar(ap(one(out)), ap(one("pi")), s1, None, op0))
+        else:
+            op("v", [one(out)], [one("pi")], lambda: g.vector.tensor_scalar(ap(one(out)), ap(one("pi")), s1, s2, op0, op1))
+    op("g", [one("pi")], [], lambda: g.iota(ap(one("pi")), [[0, 1]], 0, 1))
+    iota(R("ie"), [[16, 20]], 0, 0)
+    iota(R("j16"), [[1, 16]], 0, 0)
+    iota(R("iot"), [[1, C]], -160, 0)
+    op("g", [R("offi")], [], lambda: g.iota(ap(R("offi")), [[16, 8]], -16, 0))
+    iota(R("d0f"), [[0, 640]], 1024, 0)
+    for n in ("frf", "frb"):
+        iota(R(n, 0, 64), [[0, 64]], 0, 0)
+        iota(R(n, 704, 736), [[0, 32]], 0, 0)
+    iota(R("t1", 0, 16), [[0, 16]], 0, 0)
+    iota(R("t1", 336, 352), [[0, 16]], 0, 0)
+    iota(R("z01"), [[0, 320], [1, 2]], 0, 0)
+    iota(R("d0b"), [[0, 640]], 1024, 0)
+    iota(R("ac"), [[0, 32]], 0, 0)
+    iota(R("bc"), [[0, 32]], 0, 0)
+    iota(R("ones"), [[0, 512]], 1, 0)
+    for b in range(4):
+        o = R("et", 512 * b, 512 * b + 512)
+        op("g", [o], [R("ones")], lambda o=o, b=b: g.affine_select(ap(o), ap(R("ones")), [[-1, 512]], A.is_equal, 0.0, b, 4))
+    bits("ki", 15, A.bitwise_and)
+    bits("si", 4, A.arith_shift_right, 1, A.bitwise_and)
+    bits("p31", 31, A.bitwise_and)
+    copy(one("kf"), one("ki"))
+    copy(one("mo"), one("si"))
+    copy(one("p31f"), one("p31"))
+    ts(one("hh"), one("kf"), 15.0, A.is_lt, 512.0, A.mult)
+    ts(R("df"), R("j16"), one("kf"), A.subtract)
+    ts(R("k16"), R("ie"), 0.0, A.mult, one("kf"), A.add)
+    ts(R("ha"), R("df"), 0.0, A.is_equal, -4096.0, A.mult)
+    ts(R("hb"), R("df"), 1.0, A.is_equal, 512.0, A.mult)
+    ts(R("iwc"), R("ie"), one("kf"), A.add, 160.0, A.subtract)
+    tt(R("hc16"), R("ha"), R("hb"), A.add)
+    pick("s", R("hc"), R("hc16"), R("k16"))
+    for n, c, v in (("tw1", 0, -512.0), ("tw2", 0, 512.0)):
+        fill(R(n, 0, 1), v)
+        fill(R(n, 1, 16), -v)
+    for n, a, b in (("s1", -1.0, 2.0), ("b1", 511.0, 385.0), ("s2", 1.0, 1.0), ("b2", -543.0, 928.0), ("gg", -16.0, 1264.0), ("sgo", -16.0, 176.0)):
+        ts(one(n), one("mo"), a, A.mult, b, A.add)
+
+    copy(R("qo16"), R("gqs"))
+    copy(R("mo16"), R("gms"))
+    pick("v", R("qr"), R("iot"), R("qo16"))
+    ts(R("qf"), R("gqs"), 160.0, A.subtract)
+    ts(R("mf"), R("gms"), 160.0, A.subtract)
+    pick("v", R("qmr"), R("qr"), R("mo16"))
+    tt(R("kw"), R("iwc"), R("mf"), A.min)
+    copy(R("offu"), R("offi"))
+    unrow("qmw", "qmr")
+    fill(R("offu", 0, 1), 112)
+    quant("uq", R("ut"), 0, 128)
+    ts(R("kof"), R("kw"), 160.0, A.add)
+    op("s", [R("uss")], [R("uqs"), R("offu")], lambda: g.scalar.activation(T.uss[:, 0:128], T.uqs[:, 0:128].indirect(T.offu[:, 0:8]), F.Copy))
+
+    def tables(d, qw, qmw):
+        tt(R("tiw"), R(qmw), R(qw), A.is_gt)
+        tt(R("hiw"), R(qw), R(qmw), A.max)
+        tt(R("low"), R(qw), R(qmw), A.min)
+        copy(R("ti" + d), R("tiw"))
+        ts(R("hi" + d), R("hiw"), 160.0, A.add)
+        ts(R("lof" if d == "f" else "kob"), R("low"), 160.0, A.add)
+        pick("s", R("t" + d), R("tw1"), R("ti" + d))
+        pick("v" if d == "f" else "s", R("d1" + d, 1, 640, 2), R("iot"), R("hi" + d))
+        pick("s", R("d0" + d, 1, 640, 2), R("iot"), R("lof" if d == "f" else "kob"))
+
+    def window_list(d, kw):
+        ts(R("kta"), R("tiw"), -320.0, A.mult, 480.0, A.add)
+        tt(R("ktc"), R("kta"), R(kw), A.add)
+        copy(R("kt" + d), R("ktc"))
+
+    def signs(moving, h):
+        c0, c1 = HALVES[h]
+        mx(h, c1 - c0, "us", 0, moving, c0)
+        act(R("sg", c0, c1), R("ps%d" % h, 0, c1 - c0), F.Sign, bias=-EPS)
+
+    def halves(name, src, decide):
+        for h, (c0, c1) in enumerate(HALVES):
+            quant(name, R(src, 4 * c0, 4 * c1), c0, c1)
+            if decide:
+                signs(name, h)
+
+    op("v", [R("usc")], [R("uqc"), R("offu")], lambda: g.vector.tensor_copy(T.usc[:, 0:128].bitcast(dt.uint32), T.uqc[:, 0:128].bitcast(dt.uint32).indirect(T.offu[:, 0:8])))
+    tables("f", "qf", "qmw")
+    halves("xq", "xt", True)
+    pick("s", R("mr"), R("iot"), R("mo16"))
+
+    def ring():
+        state["bank"] += 1
+        return 2 + state["bank"] % 6
+
+    def choose(d):
+        pick_tt(R("d1" + d, 0, 640, 2), R("sg"), R("ko" + d), R("t" + d), A.mult)
+
+    def rows(d):
+        scan(R("fr" + d, 64, 704), R("d0" + d), R("d1" + d), A.max, A.min)
+
+    def place(kind, out, s, p0=0, p1=128):
+        if kind in "12":
+            ts(out, s, one("s" + kind, p0, p1), A.mult, one("b" + kind, p0, p1), A.add)
+        else:
+            ts(out, s, one(kind, p0, p1), A.add)
+
+    def lists(d, q, s, p0, p1, with_sl):
+        sl, ll = ("sl", "ll") if d == "f" else ("slb", "llb")
+        p = (32 * q, 32 * q + p1 - p0)
+        todo = [lambda: place("1" if d == "f" else "gg", R(ll, 0, 20, 2, *p), s, p0, p1), lambda: place("gg" if d == "f" else "2", R(ll, 1, 20, 2, *p), s, p0, p1)]
+        one_more = lambda: place("sgo", R(sl, 0, 10, 1, *p), s, p0, p1)
+        for f in ([one_more] if with_sl == 1 else []) + todo + ([one_more] if with_sl == 2 else []):
+            f()
+
+    def turned(q, st):
+        return R("tt", 0, 10 * st, st, 32 * q, 32 * q + 32), 32 * q, 32 * q + 32
+
+    def step(d, q, to, with_sl):
+        pick("v", R("rr"), R("fr" + d, 1088, 1440), R("sl" if d == "f" else "slb"))
+        spare()
+        turn(R("tt", 0, 160, 1, 32 * q, 32 * q + 32), R("rr", 0, 160, 1, 32 * q, 32 * q + 32))
+        spare()
+        lists(d, to, *turned(q, 16), with_sl)
+
+    def finish(d, out, crossed):
+        pick("v", R("mm"), R("fr" + d), R("ll" if d == "f" else "llb"))
+        spare()
+        turn(R("tm"), R("mm"))
+        spare()
+        ts(R(out), R("tm", 0, 320, 16), 160.0, A.add)
+        spare()
+        for q in crossed:
+            p = (32 * q, 32 * q + 32)
+            ts(R(out, 1, 20, 4, *p), R("tm", 32, 320, 64, *p), 160.0, A.add)
+            ts(R(out, 2, 20, 4, *p), R("tm", 16, 320, 64, *p), 160.0, A.add)
+
+    def compose(d, between):
+        fr, o = "fr" + d, 0 if d == "f" else 16
+        turn(R("t1", 16, 336), R(fr, 65, 704, 2))
+        turn(R("t1p"), R(fr, 33, 736, 2))
+        turn(R(fr, 736, 1088), R("t1"))
+        k = "2" if d == "f" else "1"
+        place(k, R("fl", 0, 22, 2), R("t1p", o, 352, 32))
+        place(k, R("fl", 1, 20, 2), R("t1", 16 + o, 336, 32))
+        between()
+        pick("v", R(fr, 1088, 1440), R(fr, 0, 1088), R("fl"))
+        spare()
+
+    def planes(src):
+        for t in range(4):
+            act(R("xp", C * t, C * t + C), R(src, t, 1280, 4), F.Copy, scale=0.5)
+            act(R("xi", C * t, C * t + C) if t < 3 else R("ys", 0, 640, 2), R(src, t, 1280, 4), F.Copy, scale=0.5)
+
+    def passes(out, win, off, other, pairs, between):
+        def fused(t):
+            pick_tt(R(out, t, 1280, 4), R(win, C * t, C * t + C), R(off), other(t), A.add)
+        pick("s", R(pairs, 1, 640, 2), R(win, 960, 1280), R(off))
+        fused(0)
+        between[0]()
+        scan(R(out, 1, 1280, 2), R("z01"), R(pairs), A.mult, A.add)
+        between[1]()
+        fused(2)
+        fused(1)
+
+    ts(R("vf"), R("ie", 0, 10), 2.0, A.mult, one("p31f"), A.add)
+    fill(R("fl", 20, 22), 0)
+    ts(R("vf"), R("vf"), 160.0, A.subtract)
+    lists("f", 0, R("vf"), 0, 128, 1)
+    window_list("f", "kw")
+    waiting += [
+        lambda: op("v", [R("qir")], [R("qo16"), R("iot")], lambda: g.vector.tensor_copy(ap(R("qir")).indirect(ap(R("qo16"))), ap(R("iot")))),
+        lambda: unrow("qiw", "qir"),
+        lambda: ts(R("qio"), R("qiw"), 160.0, A.add),
+        lambda: (pick("s", R("mqr"), R("mr"), R("qio")), planes("xt")),
+        lambda: lists("b", 0, R("vf"), 0, 128, 1),
+        lambda: copy(R("ac", 0, 20), R("iwc")),
+        lambda: unrow("mqw", "mqr"),
+        lambda: turn(R("at"), R("ac")),
+        lambda: tables("b", "qiw", "mqw"),
+        lambda: copy(R("a2", 0, 16, 1, 0, 32), R("at", 0, 16, 1, 0, 32)),
+        lambda: window_list("b", "low")]
+
+    def nothing():
+        pass
+
+    for rnd, s in enumerate(ROUNDS):
+        peer = T.cores[rank ^ s]
+        rid, pid, _se = topo.addr(peer)
+        mask, neng = topo.mask(core, peer), len(topo.engines(core, peer))
+        choose("f")
+        spare()
+        rows("f")
+        spare()
+        compose("f", spare)
+        turn(R("tt", 0, 320, 1, 0, 32), R("frf", 1104, 1424, 1, 0, 32))
+        spare()
+        lists("f", 1, *turned(0, 32), 1)
+        step("f", 1, 2, 1)
+        step("f", 2, 3, 2)
+        finish("f", "xo", (2,))
+        while waiting:
+            spare()
+        passes("vt", "xp", "xo", lambda t: R("xi", C * t, C * t + C), "ys", (nothing, nothing))
+        halves("vq", "vt", True)
+        for h, (c0, c1) in enumerate(HALVES):
+            for b in range(4):
+                k = ring()
+                mx(k, c1 - c0, "wq", 128 * b, "vq", c0)
+                act(R("ht", 4 * c0 + b, 4 * c1, 4), R("ps%d" % k, 0, c1 - c0), F.Copy, scale=0.03125)
+        act(R("yv", 0, 640, 2), R("vt", 3, 1280, 4), F.Copy)
+        pick("v", R("rr8"), R("frf", 1088, 1440), R("sl"))
+        ts(R("ac", 0, 20), R("xo"), 160.0, A.subtract)
+        turn(R("tt", 0, 160, 1, 96, 128), R("rr8", 0, 160, 1, 96, 128))
+        turn(R("at"), R("ac"))
+        lists("b", 3, *turned(3, 16), 1)
+        if rnd == 0:
+            quant("vvq", R("vv"), 0, 128)
+        waiting.append(lambda: copy(R("a2", 16, 32), R("at", 0, 16)))
+        waiting += [lambda q=q: copy(R("a2", 0, 16, 1, 32 * q + 32, 32 * q + 64), R("at", 16, 32, 1, 32 * q, 32 * q + 32)) for q in range(3)]
+
+        def send(h):
+            c0, c1 = C * rnd + HALVES[h][0], C * rnd + HALVES[h][1]
+            quant("hq", R("ht", 4 * HALVES[h][0], 4 * HALVES[h][1]), c0, c1)
+            order("g", [], [R("hqc", c0, c1), R("hqs", c0, c1)])
+            sem = "ar%d_%d" % (rnd, h)
+            g.remote_dma(T.rqc[:, c0:c1].bitcast(dt.uint8), T.hqc[:, c0:c1].bitcast(dt.uint8), T.sem[sem], T.sem.lsem, pid, rid, mask)
+            g.remote_dma(T.rqs[:, c0:c1], T.hqs[:, c0:c1], T.sem[sem], T.sem.lsem, pid, rid, mask)
+            pending["lsem"] = pending.get("lsem", 0) + 2 * neng
+            pending[sem] = 2 * neng
+            clock[(sem, 2 * neng)] = {}
+            note([R("rqc", c0, c1), R("rqs", c0, c1)], [], (sem, 2 * neng))
+
+        choose("b")
+        spare()
+        rows("b")
+        send(0)
+        compose("b", lambda: send(1))
+        step("b", 3, 2, 1)
+        step("b", 2, 1, 1)
+        if rnd == 0:
+            quant("eq", R("et"), 0, 512)
+        step("b", 1, 0, 0)
+        for h, (c0, c1) in enumerate(HALVES):
+            for b in range(4):
+                k = ring()
+                mx(k, c1 - c0, "eq", 128 * b, "rq", C * rnd + c0)
+                act(R("dp", C * b + c0, C * b + c1), R("ps%d" % k, 0, c1 - c0), F.Copy)
+        finish("b", "xob", (1, 3))
+        while waiting:
+            spare()
+        xn = "xn%d" % rnd
+        last = rnd == 2
+
+        def misses():
+            cu, old = "cu%d" % (rnd % 2), "cu%d" % (1 - rnd % 2)
+            tt(R("md" if rnd else cu), R("a2"), R("bt"), A.not_equal)
+            if rnd:
+                tt(R(cu), R(old), R("md"), A.not_equal)
+            turn(R("cut"), R(cu))
+            copy(R("moff"), R("cut"))
+            a, b = (320, 0) if last else (0, 320)
+            pick("s", R("w", a, a + 320), R("tw2"), R("moff", 0, 20))
+            act(R("w", b, b + 320), R("w", a, a + 320), F.Copy, scale=-1.0)
+            pick("s", R("d1f", 0, 640, 2) if last else R("tf"), R("w"), R("ktf"))
+        ts(R("bc", 0, 20), R("xob"), 160.0, A.subtract)
+        passes(xn, "dp", "xob", lambda t: R("vt", t, 1280, 4), "yv", (lambda: turn(R("bt"), R("bc")), misses))
+        halves("xq", xn, not last)
+        if not last:
+            planes(xn)
+            pick("s", R("tb"), R("w"), R("ktb"))
+
+    for h, (c0, c1) in enumerate(HALVES):
+        mx(h, c1 - c0, "vvq", 0, "xq", c0)
+        copy(R("yt", c0, c1), R("ps%d" % h, 0, c1 - c0))
+        dma("y", [], [R("yt", c0, c1)], T.y[:, c0:c1], ap(R("yt", c0, c1)))
+    rows("f")
+    act(R("qout"), R("frf", 65, 704, 2), F.Identity, bias=160.0)
+    dma("s", [], [R("qout")], T.qo[:, :], T.qout[0:128:16, :])
+    dma("y", [], [R("xqc")], T.oc[:, :], T.xqc[:, :].bitcast(dt.uint8))
+    for k in range(4):
+        dma("y", [], [R("xqs")], T.osc[4 * k:4 * k + 4, :], T.xqs[32 * k:32 * k + 4, :])
+    for sem, val in sorted(pending.items()):
+        g.wait_ge(T.sem[sem], val)
+    for sem, val in count.items():
+        g.wait_ge(T.sem[sem], val)

@@ -3,7 +3,7 @@ from concourse.mybir import dt, AluOpType as A, ActivationFunctionType as F
 C = 320
 ROUNDS = (1, 2, 4)
 HALVES = ((0, 160), (160, 320))
-EPS = 2.0 ** -93
+BIG = 1e29
 
 SCRATCH = {}
 
@@ -13,13 +13,14 @@ def _buf(dtype, **widths):
         SCRATCH[k] = ("sbuf", [128, n], dtype)
 
 
-_buf("bfloat16", xt=1280, xn0=1280, xn1=1280, xn2=1280, xp=1280, xi=960, vt=1280, ht=1280, dp=1280, ut=512, vv=512, et=2048, ones=512,
-     iot=320, hs=80, hc=320, tw=48, z01=640, ys=640, yv=640, qr=320, qmr=320, qir=320, mr=320, mqr=320, d0f=640, d1f=640, d0b=640, d1b=640,
-     tf=320, tb=320, w=640, sg=320, frf=1440, frb=1440, t1=352, t1p=352, tt=320, rr=160, rr8=160, mm=320, tm=320,
-     ac=32, at=32, a2=32, bc=32, bt=32, md=32, cu0=32, cu1=32, cut=32)
-_buf("float32", sm=120, ie=20, col=16, iwc=20, vf=10, qf=20, mf=20, qmw=20, qiw=20, mqw=20, wm=320, qout=320, yt=320)
-_buf("int32", icol=4, offi=8, gqs=20, gms=20)
-_buf("uint16", offu=8, k16=20, qo16=20, mo16=20, qio=20, kof=20, kob=20, lof=20, hif=20, tif=20, hib=20, tib=20, fl=22, sl=10, slb=10, ll=20, llb=20, xo=20, xob=20, moff=32, ktf=20, ktb=20)
+_buf("bfloat16", xt=1280, xn0=1280, xn1=1280, xn2=1280, xp=1280, vt=1280, ht=1280, dp=1280, ut=512, vv=512, et=2048, ones=512,
+     iot=320, xi=960, tw=16, z01=640, ys=640, yv=640, qr=320, rw=1280, rt=1280, bl=320, sc=320, rb2=640, tb2=640,
+     wb=960, sgb=320, rf=320, rb=320, pk=320, t0=320, m1=80, nn=320, nw=320, g1=160, t2=320, gw=320, zw=480, t3=192, fr=192, xf=352, xb=352,
+     aa=96, md=64, cu0=64, cu1=64, km=30, q0=960, q1=960, q2=960)
+_buf("float32", col=32, fb=8, sm=48, ie=20, iw=96, i40=40, ef=160, eb=160, qout=320, yt=320)
+_buf("int32", ib=8, gg=96, iwi=20)
+_buf("uint16", offu=8, qo16=20, mo16=20, pl=10, la=96, lb=64, kf=20, kb=20, krf=20, krb=20, kn=20, l1=10, l2f=10, l2b=10, l3f=10, l3b=10,
+     sef=2, seb=2, al=6, bm=4, xo=32, xob=32, moff=64)
 for _n, _w in (("uq", 128), ("us", 128), ("xq", 320), ("vq", 320), ("vvq", 128), ("eq", 512), ("wq", 512), ("hq", 960), ("rq", 960)):
     SCRATCH[_n + "c"] = ("sbuf", [128, _w], "float8_e4m3fn_x4")
     SCRATCH[_n + "s"] = ("sbuf", [128, _w], "uint8")
@@ -29,11 +30,13 @@ for _b in range(8):
 NDMA = 20
 SEMAPHORES = ["qv", "qs", "qt", "qg", "lsem"] + ["d%d" % i for i in range(NDMA)] + ["ar%d_%d" % (r, h) for r in range(3) for h in range(2)]
 
-PLACE = {"tw1": ("tw", 0, 16), "tw2": ("tw", 32, 16)}
-PLACE.update({n: ("col", i, 1) for i, n in enumerate(("kf", "mo", "hh", "p31f", "s1", "b1", "s2", "b2", "gg", "sgo"))})
-PLACE.update({n: ("icol", i, 1) for i, n in enumerate(("pi", "ki", "si", "p31"))})
-PLACE.update({n: ("hs", 16 * i, 16) for i, n in enumerate(("j16", "df", "ha", "hb", "hc16"))})
-PLACE.update({n: ("sm", 20 * i, 20) for i, n in enumerate(("kw", "low", "hiw", "tiw", "kta", "ktc"))})
+PLACE = {n: ("fb", i, 1) for i, n in enumerate(("b0", "b0x", "b1", "r", "r2", "r4", "d", "g3"))}
+PLACE.update({n: ("col", i, 1) for i, n in enumerate(("thr", "cs", "rs", "rz", "dl", "xa", "xc", "rd", "p31", "zo", "u16", "lowe", "lowo", "cx", "d160",
+                                                      "rof", "rob", "mb", "fn", "im", "ic", "c1", "c2", "c3", "kp"))})
+PLACE.update({n: ("sm", 2 * i, 2) for i, n in enumerate(("cS", "cH", "fS", "fH", "t1", "cA", "cB", "m2", "jn", "ge", "j16", "base"))})
+PLACE.update({"i3": ("sm", 24, 10), "w2": ("wb", 0, 640), "sgf": ("wb", 640, 320), "km3": ("km", 20, 10),
+              "e1f": ("ef", 0, 80), "e2f": ("ef", 80, 80), "e1b": ("eb", 0, 80), "e2b": ("eb", 80, 80)})
+ENTRY, FIRST, MATE, BOTH = 1, 2, 4, 8
 
 
 def R(name, c0=0, c1=None, st=1, p0=0, p1=128):
@@ -82,7 +85,7 @@ def rank_program(g, core, T, topo):
             ev |= {e for w, e in writes.get(r[0], []) if hit(r, w)}
         for r in outs:
             ev |= {e for w, e in writes.get(r[0], []) if hit(r, w)}
-            ev |= {e for w, e in reads.get(r[0], []) if hit(r, w) and e[0] != "q" + q}
+            ev |= {e for w, e in reads.get(r[0], []) if hit(r, w)}
         settle(q, ev)
 
     def note(outs, ins, ev):
@@ -112,26 +115,31 @@ def rank_program(g, core, T, topo):
         pending[sem] = 16
         note(outs, ins, (sem, 16))
 
+    def arg(s):
+        return ap(s) if isinstance(s, tuple) else s
+
+    def cols(*ss):
+        return [s for s in ss if isinstance(s, tuple)]
+
     def copy(out, src):
         op("v", [out], [src], lambda: g.vector.tensor_copy(ap(out), ap(src)))
 
-    def pick(q, out, win, off):
-        if q == "v":
-            op(q, [out], [win, off], lambda: g.vector.tensor_copy(ap(out), ap(win).indirect(ap(off))))
-        else:
-            op(q, [out], [win, off], lambda: g.scalar.activation(ap(out), ap(win).indirect(ap(off)), F.Copy))
+    def pick(out, win, off):
+        op("v", [out], [win, off], lambda: g.vector.tensor_copy(ap(out), ap(win).indirect(ap(off))))
 
     def pick_tt(out, win, off, other, alu):
         op("v", [out], [win, off, other], lambda: g.vector.tensor_tensor(ap(out), ap(win).indirect(ap(off)), ap(other), alu))
 
-    def ts(out, src, s1, op0, s2=None, op1=None):
-        col = [s for s in (s1, s2) if isinstance(s, tuple)]
-        a1 = ap(s1) if isinstance(s1, tuple) else s1
-        a2 = ap(s2) if isinstance(s2, tuple) else s2
-        if op1 is None:
-            op("v", [out], [src] + col, lambda: g.vector.tensor_scalar(ap(out), ap(src), a1, None, op0))
-        else:
-            op("v", [out], [src] + col, lambda: g.vector.tensor_scalar(ap(out), ap(src), a1, a2, op0, op1))
+    def ts(out, src, s1, op0, s2=None, op1=None, off=None):
+        def call():
+            a = ap(src) if off is None else ap(src).indirect(ap(off))
+            if op1 is None:
+                return g.vector.tensor_scalar(ap(out), a, arg(s1), None, op0)
+            return g.vector.tensor_scalar(ap(out), a, arg(s1), arg(s2), op0, op1)
+        op("v", [out], [src] + cols(s1, s2, off), call)
+
+    def lin(out, src, a, b, off=None):
+        ts(out, src, a, A.mult, b, A.add, off)
 
     def tt(out, a, b, alu):
         op("v", [out], [a, b], lambda: g.vector.tensor_tensor(ap(out), ap(a), ap(b), alu))
@@ -139,14 +147,17 @@ def rank_program(g, core, T, topo):
     def fill(out, val):
         op("v", [out], [], lambda: g.vector.memset(ap(out), val))
 
-    def iota(out, pattern, base, cm):
-        op("g", [out], [], lambda: g.iota(ap(out), pattern, base, cm, allow_small_or_imprecise_dtypes=True))
+    def iota(out, pattern, base, cm=0):
+        if SCRATCH[out[0]][2] == "int32":
+            op("g", [out], [], lambda: g.iota(ap(out), pattern, base, cm))
+        else:
+            op("g", [out], [], lambda: g.iota(ap(out), pattern, base, cm, allow_small_or_imprecise_dtypes=True))
 
     def turn(out, src):
         op("v", [out], [src], lambda: g.vector.transpose(ap(out), ap(src)))
 
-    def scan(out, d0, d1, op0, op1):
-        op("v", [out], [d0, d1], lambda: g.vector.tensor_tensor_scan(ap(out), ap(d0), ap(d1), 0.0, op0, op1))
+    def scan(out, d0, d1):
+        op("v", [out], [d0, d1], lambda: g.vector.tensor_tensor_scan(ap(out), ap(d0), ap(d1), 0.0, A.mult, A.add))
 
     def quant(name, src, c0, c1):
         o, s = R(name + "c", c0, c1), R(name + "s", c0, c1)
@@ -157,21 +168,26 @@ def rank_program(g, core, T, topo):
         o = R("ps%d" % bank, 0, n)
         op("t", [R("ps%d" % bank)], [w, ws, m, ms], lambda: g.tensor.matmul_mx(ap(o), ap(w), ap(ws), ap(m), ap(ms), True, True))
 
-    def act(out, src, func, scale=1.0, bias=0.0):
-        op("s", [out], [src], lambda: g.scalar.activation(ap(out), ap(src), func, bias=bias, scale=scale))
+    def act(out, src, scale=1.0, bias=0.0, off=None):
+        func = F.Copy if bias == 0.0 else F.Identity
+        op("s", [out], [src] + cols(scale, bias, off),
+           lambda: g.scalar.activation(ap(out), ap(src) if off is None else ap(src).indirect(ap(off)), func, bias=arg(bias), scale=arg(scale)))
 
-    def unrow(dst, src):
-        scan(R("wm"), R("hc"), R(src), A.add, A.max)
-        ts(R(dst), R("wm", 15, 320, 16), one("hh"), A.subtract)
+    def quad(q):
+        return 32 * q, 32 * q + 32
+
+    def one(n, q=None):
+        return R(n, 0, 1) if q is None else R(n, 0, 1, 1, *quad(q))
 
     waiting = []
 
-    def spare():
-        if waiting:
-            waiting.pop(0)()
+    def spare(n=1):
+        for _ in range(n):
+            if waiting:
+                waiting.pop(0)()
 
-    dma("y", [R("gqs")], [], ap(R("gqs")), T.gq[:, :])
-    dma("y", [R("gms")], [], ap(R("gms")), T.gm[:, :])
+    dma("y", [R("gg", 0, 20)], [], ap(R("gg", 0, 20)), T.gq[:, :])
+    dma("y", [R("gg", 32, 52)], [], ap(R("gg", 32, 52)), T.gm[:, :])
     dma("y", [R("xt")], [], ap(R("xt")), T.x[:, :])
     dma("s", [R("ut")], [], ap(R("ut")), T.u[:, :])
     order("y", [], [R("xt")])
@@ -179,228 +195,277 @@ def rank_program(g, core, T, topo):
     dma("y", [R("wqs")], [], T.wqs[:, :], T.ws[:, :])
     dma("y", [R("vv")], [], ap(R("vv")), T.v[:, :])
 
-    def one(n, p0=0, p1=128):
-        return R(n, 0, 1, 1, p0, p1)
-
-    def bits(out, s1, op0, s2=None, op1=None):
-        if op1 is None:
-            op("v", [one(out)], [one("pi")], lambda: g.vector.tensor_scalar(ap(one(out)), ap(one("pi")), s1, None, op0))
-        else:
-            op("v", [one(out)], [one("pi")], lambda: g.vector.tensor_scalar(ap(one(out)), ap(one("pi")), s1, s2, op0, op1))
-    op("g", [one("pi")], [], lambda: g.iota(ap(one("pi")), [[0, 1]], 0, 1))
-    iota(R("ie"), [[16, 20]], 0, 0)
-    iota(R("j16"), [[1, 16]], 0, 0)
-    iota(R("iot"), [[1, C]], -160, 0)
-    op("g", [R("offi")], [], lambda: g.iota(ap(R("offi")), [[16, 8]], -16, 0))
-    iota(R("d0f"), [[0, 640]], 1024, 0)
-    for n in ("frf", "frb"):
-        iota(R(n, 0, 64), [[0, 64]], 0, 0)
-        iota(R(n, 704, 736), [[0, 32]], 0, 0)
-    iota(R("t1", 0, 16), [[0, 16]], 0, 0)
-    iota(R("t1", 336, 352), [[0, 16]], 0, 0)
-    iota(R("z01"), [[0, 320], [1, 2]], 0, 0)
-    iota(R("d0b"), [[0, 640]], 1024, 0)
-    iota(R("ac"), [[0, 32]], 0, 0)
-    iota(R("bc"), [[0, 32]], 0, 0)
-    iota(R("ones"), [[0, 512]], 1, 0)
+    iota(R("iwi", 0, 2), [[0, 2]], 0, 1)
+    iota(R("ie"), [[16, 20]], 0)
+    iota(R("sm", 0, 4), [[-2, 2], [-1, 2]], 2)
+    iota(R("sm", 36, 44), [[32, 4], [0, 2]], -16)
+    iota(R("iot"), [[1, C]], -160)
+    iota(R("ef"), [[0, 160]], 0)
+    iota(R("i40"), [[64, 10], [0, 4]], 0)
+    iota(R("nn"), [[0, 320]], 0)
+    iota(R("t2"), [[0, 320]], 0)
+    iota(R("i3"), [[32, 5], [160, 2]], 0)
+    iota(R("bl"), [[1, C]], -160)
+    for n in ("t3", "fr"):
+        iota(R(n), [[0, 192]], 0)
+    iota(R("iw"), [[0, 3], [16, 32]], 0)
+    iota(R("eb"), [[0, 160]], 0)
+    iota(R("z01"), [[0, 320], [1, 2]], 0)
+    iota(R("ones"), [[0, 512]], 1)
     for b in range(4):
         o = R("et", 512 * b, 512 * b + 512)
         op("g", [o], [R("ones")], lambda o=o, b=b: g.affine_select(ap(o), ap(R("ones")), [[-1, 512]], A.is_equal, 0.0, b, 4))
-    bits("ki", 15, A.bitwise_and)
-    bits("si", 4, A.arith_shift_right, 1, A.bitwise_and)
-    bits("p31", 31, A.bitwise_and)
-    copy(one("kf"), one("ki"))
-    copy(one("mo"), one("si"))
-    copy(one("p31f"), one("p31"))
-    ts(one("hh"), one("kf"), 15.0, A.is_lt, 512.0, A.mult)
-    ts(R("df"), R("j16"), one("kf"), A.subtract)
-    ts(R("k16"), R("ie"), 0.0, A.mult, one("kf"), A.add)
-    ts(R("ha"), R("df"), 0.0, A.is_equal, -4096.0, A.mult)
-    ts(R("hb"), R("df"), 1.0, A.is_equal, 512.0, A.mult)
-    ts(R("iwc"), R("ie"), one("kf"), A.add, 160.0, A.subtract)
-    tt(R("hc16"), R("ha"), R("hb"), A.add)
-    pick("s", R("hc"), R("hc16"), R("k16"))
-    for n, c, v in (("tw1", 0, -512.0), ("tw2", 0, 512.0)):
-        fill(R(n, 0, 1), v)
-        fill(R(n, 1, 16), -v)
-    for n, a, b in (("s1", -1.0, 2.0), ("b1", 511.0, 385.0), ("s2", 1.0, 1.0), ("b2", -543.0, 928.0), ("gg", -16.0, 1264.0), ("sgo", -16.0, 176.0)):
-        ts(one(n), one("mo"), a, A.mult, b, A.add)
+    iota(R("q0"), [[0, 320], [1, 3]], 0)
 
-    copy(R("qo16"), R("gqs"))
-    copy(R("mo16"), R("gms"))
-    pick("v", R("qr"), R("iot"), R("qo16"))
-    ts(R("qf"), R("gqs"), 160.0, A.subtract)
-    ts(R("mf"), R("gms"), 160.0, A.subtract)
-    pick("v", R("qmr"), R("qr"), R("mo16"))
-    tt(R("kw"), R("iwc"), R("mf"), A.min)
-    copy(R("offu"), R("offi"))
-    unrow("qmw", "qmr")
-    fill(R("offu", 0, 1), 112)
+    for c0, c1 in ((20, 32), (52, 64), (84, 96)):
+        fill(R("gg", c0, c1), 0)
+    for c0, c1, sh, mask in ((0, 2, 0, 1), (2, 3, 1, 1), (3, 4, 0, 15), (4, 5, 1, 7), (5, 6, 2, 3), (6, 7, 4, 1), (7, 8, 4, 3)):
+        ts(R("ib", c0, c1), R("iwi", 0, c1 - c0), sh, A.arith_shift_right, mask, A.bitwise_and)
+    fill(R("cH", 1, 2), 3.0)
+    copy(R("fb"), R("ib"))
+    act(one("u16"), one("b0"), 16.0)
+    act(one("thr"), one("r2"), -BIG, BIG)
+    act(one("p31"), one("d"), 16.0, one("r"))
+    act(one("zo"), one("d"), -160.0, 320.0)
+    act(one("cx"), one("d"), -352.0, 32.0)
+    act(one("fn"), one("p31"), 2.0, -320.0)
+    ts(one("dl"), one("b0"), one("b1"), A.subtract)
+    ts(one("c1"), one("r4"), -2.0, A.mult)
+    ts(R("fS", 0, 4), R("cS", 0, 4), one("g3"), A.is_equal)
+    lin(one("xa"), one("b1"), 8.0, one("c1"))
+    lin(one("xc"), one("b0"), 8.0, one("c1"))
+    ts(one("rd"), one("r"), one("dl"), A.add, 64.0, A.add)
+    ts(R("t1"), R("fS"), one("dl"), A.mult)
+    lin(R("cA"), R("fH"), one("xa"), one("r"))
+    lin(R("cB"), R("fH"), one("xc"), one("rd"))
+    lin(R("m2"), R("fH"), -0.5, 1.0)
+    tt(R("cA"), R("cA"), R("t1"), A.add)
+    tt(R("cB"), R("cB"), R("t1"), A.subtract)
+    copy(R("qo16"), R("gg", 0, 20))
+    ts(R("iwi"), R("ie"), one("r"), A.add)
+    act(R("qr"), R("iot"), off=R("qo16"))
+    lin(R("pl", 0, 2), R("ie", 0, 2), R("m2", 0, 1), R("cA", 0, 1))
+    lin(R("pl", 4, 6), R("ie", 0, 2), R("m2", 0, 1), R("cB", 0, 1))
+    tt(R("gg", 64, 84), R("gg", 32, 52), R("iwi"), A.min)
+    ts(R("pl", 2, 4), R("pl", 0, 2), 32.0, A.add)
+    ts(R("offu"), R("sm", 36, 44), one("u16"), A.add)
     quant("uq", R("ut"), 0, 128)
-    ts(R("kof"), R("kw"), 160.0, A.add)
+
+    ts(R("la"), R("gg"), 0.0, A.add, off=R("pl", 0, 6))
+    lin(R("offu", 0, 2), R("fb", 0, 2), -112.0, 112.0)
+    copy(R("mo16"), R("gg", 32, 52))
+    act(R("rw", 640, 960), R("iot"), off=R("la", 64, 84))
     op("s", [R("uss")], [R("uqs"), R("offu")], lambda: g.scalar.activation(T.uss[:, 0:128], T.uqs[:, 0:128].indirect(T.offu[:, 0:8]), F.Copy))
+    act(R("rw", 0, 320), R("iot"), off=R("la", 0, 20))
+    act(R("rw", 960, 1280), R("iot"), off=R("mo16"))
+    op("v", [R("usc")], [R("uqc"), R("offu")], lambda: g.vector.tensor_copy(T.usc[:, 0:128].bitcast(dt.uint32), T.uqc[:, 0:128].bitcast(dt.uint32).indirect(T.offu[:, 0:8])))
+    dma("y", [R("bl")], [R("rw", 960, 1280)], T.bl[1:128:2, :], T.rw[1:128:2, 960:1280])
 
-    def tables(d, qw, qmw):
-        tt(R("tiw"), R(qmw), R(qw), A.is_gt)
-        tt(R("hiw"), R(qw), R(qmw), A.max)
-        tt(R("low"), R(qw), R(qmw), A.min)
-        copy(R("ti" + d), R("tiw"))
-        ts(R("hi" + d), R("hiw"), 160.0, A.add)
-        ts(R("lof" if d == "f" else "kob"), R("low"), 160.0, A.add)
-        pick("s", R("t" + d), R("tw1"), R("ti" + d))
-        pick("v" if d == "f" else "s", R("d1" + d, 1, 640, 2), R("iot"), R("hi" + d))
-        pick("s", R("d0" + d, 1, 640, 2), R("iot"), R("lof" if d == "f" else "kob"))
-
-    def window_list(d, kw):
-        ts(R("kta"), R("tiw"), -320.0, A.mult, 480.0, A.add)
-        tt(R("ktc"), R("kta"), R(kw), A.add)
-        copy(R("kt" + d), R("ktc"))
-
-    def signs(moving, h):
+    def signs(name, h):
         c0, c1 = HALVES[h]
-        mx(h, c1 - c0, "us", 0, moving, c0)
-        act(R("sg", c0, c1), R("ps%d" % h, 0, c1 - c0), F.Sign, bias=-EPS)
+        ts(R(name, c0, c1), R("ps%d" % h, 0, c1 - c0), one("thr"), A.is_gt, one("cs"), A.subtract)
 
     def halves(name, src, decide):
         for h, (c0, c1) in enumerate(HALVES):
             quant(name, R(src, 4 * c0, 4 * c1), c0, c1)
             if decide:
-                signs(name, h)
+                mx(h, c1 - c0, "us", 0, name, c0)
 
-    op("v", [R("usc")], [R("uqc"), R("offu")], lambda: g.vector.tensor_copy(T.usc[:, 0:128].bitcast(dt.uint32), T.uqc[:, 0:128].bitcast(dt.uint32).indirect(T.offu[:, 0:8])))
-    tables("f", "qf", "qmw")
+    def tables(d, src, no, yes):
+        for e, h in (("e1" + d, 0 if d == "f" else 16), ("e2" + d, 16 if d == "f" else 0)):
+            tt(R(e, 0, 80, 8), R(src, yes + h, yes + 320 - yes % 16, 32), R(src, no + h, no + 320, 32), A.subtract)
+            tt(R(e, 1, 80, 8), R(src, yes + h, yes + 320 - yes % 16, 32), R(src, no + h, no + 320, 32), A.add)
+
     halves("xq", "xt", True)
-    pick("s", R("mr"), R("iot"), R("mo16"))
+    pick(R("rw", 320, 640), R("qr"), R("la", 32, 52))
+    turn(R("rt", 640, 960), R("rw", 640, 960))
+    ts(one("cs"), one("r2"), 1.0, A.min, 0.5, A.mult)
+    ts(one("c2"), one("g3"), 2.0, A.is_lt, 288.0, A.mult)
+    ts(R("kf", 0, 10), R("rt", 640, 960, 32), 160.0, A.add)
+    ts(R("kf", 10, 20), R("rt", 656, 960, 32), 160.0, A.add)
+    signs("sgf", 0)
+    signs("sgf", 1)
+    turn(R("rt", 0, 640), R("rw", 0, 640))
 
     def ring():
         state["bank"] += 1
         return 2 + state["bank"] % 6
 
-    def choose(d):
-        pick_tt(R("d1" + d, 0, 640, 2), R("sg"), R("ko" + d), R("t" + d), A.mult)
-
-    def rows(d):
-        scan(R("fr" + d, 64, 704), R("d0" + d), R("d1" + d), A.max, A.min)
-
-    def place(kind, out, s, p0=0, p1=128):
-        if kind in "12":
-            ts(out, s, one("s" + kind, p0, p1), A.mult, one("b" + kind, p0, p1), A.add)
+    def chain(rnd, d, between):
+        first, hops, src, to = (0, ((0, 1), (2, 3)), 1, (2, 3)) if d == "f" else (1, ((3, 2), (1, 0)), 2, (1, 0))
+        if d == "f" and rnd == 0:
+            lin(R("pk"), R("sgf"), 2.0, 0.0, off=R("kf"))
         else:
-            ts(out, s, one(kind, p0, p1), A.add)
-
-    def lists(d, q, s, p0, p1, with_sl):
-        sl, ll = ("sl", "ll") if d == "f" else ("slb", "llb")
-        p = (32 * q, 32 * q + p1 - p0)
-        todo = [lambda: place("1" if d == "f" else "gg", R(ll, 0, 20, 2, *p), s, p0, p1), lambda: place("gg" if d == "f" else "2", R(ll, 1, 20, 2, *p), s, p0, p1)]
-        one_more = lambda: place("sgo", R(sl, 0, 10, 1, *p), s, p0, p1)
-        for f in ([one_more] if with_sl == 1 else []) + todo + ([one_more] if with_sl == 2 else []):
-            f()
-
-    def turned(q, st):
-        return R("tt", 0, 10 * st, st, 32 * q, 32 * q + 32), 32 * q, 32 * q + 32
-
-    def step(d, q, to, with_sl):
-        pick("v", R("rr"), R("fr" + d, 1088, 1440), R("sl" if d == "f" else "slb"))
-        spare()
-        turn(R("tt", 0, 160, 1, 32 * q, 32 * q + 32), R("rr", 0, 160, 1, 32 * q, 32 * q + 32))
-        spare()
-        lists(d, to, *turned(q, 16), with_sl)
-
-    def finish(d, out, crossed):
-        pick("v", R("mm"), R("fr" + d), R("ll" if d == "f" else "llb"))
-        spare()
-        turn(R("tm"), R("mm"))
-        spare()
-        ts(R(out), R("tm", 0, 320, 16), 160.0, A.add)
-        spare()
-        for q in crossed:
-            p = (32 * q, 32 * q + 32)
-            ts(R(out, 1, 20, 4, *p), R("tm", 32, 320, 64, *p), 160.0, A.add)
-            ts(R(out, 2, 20, 4, *p), R("tm", 16, 320, 64, *p), 160.0, A.add)
-
-    def compose(d, between):
-        fr, o = "fr" + d, 0 if d == "f" else 16
-        turn(R("t1", 16, 336), R(fr, 65, 704, 2))
-        turn(R("t1p"), R(fr, 33, 736, 2))
-        turn(R(fr, 736, 1088), R("t1"))
-        k = "2" if d == "f" else "1"
-        place(k, R("fl", 0, 22, 2), R("t1p", o, 352, 32))
-        place(k, R("fl", 1, 20, 2), R("t1", 16 + o, 336, 32))
-        between()
-        pick("v", R(fr, 1088, 1440), R(fr, 0, 1088), R("fl"))
-        spare()
+            pick_tt(R("pk"), R("sg" + d), R("k" + d), R("r" + d), A.mult)
+        between[0]()
+        turn(R("t0"), R("pk"))
+        between[1]()
+        scan(R("nn", 0, 320, 4), R("t0", 161 - first, 320, 2), R("e2" + d))
+        scan(R("m1"), R("t0", first, 160, 2), R("e1" + d))
+        turn(R("nw"), R("nn"))
+        lin(R("l1"), R("m1", 1, 80, 8), 0.5 if d == "f" else one("mb"), 160.0)
+        between[2]()
+        pick(R("g1"), R("nw"), R("l1"))
+        between[3]()
+        turn(R("t2", 0, 320, 2), R("g1"))
+        between[4]()
+        turn(R("gw"), R("t2"))
+        for a, b in hops:
+            lin(R("l2" + d, 0, 10, 1, *quad(b)), R("t2", BOTH, 320, 32, *quad(a)), 0.5, 160.0)
+        pick(R("zw", 160, 320), R("gw"), R("l2" + d))
+        between[5]()
+        turn(R("t3", 16, 176), R("zw", 160, 320))
+        between[6]()
+        turn(R("zw", 0, 160), R("t3", 0, 160))
+        turn(R("zw", 320, 480), R("t3", 32, 192))
+        for b in to:
+            lin(R("l3" + d, 0, 10, 1, *quad(b)), R("t3", 16 + BOTH, 176, 16, *quad(src)), 0.5, one("zo", src))
+        pick(R("fr", 16, 176), R("zw"), R("l3" + d))
+        between[7]()
+        turn(R("x" + d, 0, 160), R("fr", 16, 176))
+        turn(R("x" + d, 160, 352), R("fr"))
+        between[8]()
+        lin(R("xo" if d == "f" else "xob"), R("x" + d), 0.5, 160.0, off=R("se" + d))
 
     def planes(src):
         for t in range(4):
-            act(R("xp", C * t, C * t + C), R(src, t, 1280, 4), F.Copy, scale=0.5)
-            act(R("xi", C * t, C * t + C) if t < 3 else R("ys", 0, 640, 2), R(src, t, 1280, 4), F.Copy, scale=0.5)
+            act(R("xp", C * t, C * t + C), R(src, t, 1280, 4), 0.5)
+            act(R("xi", C * t, C * t + C) if t < 3 else R("ys", 0, 640, 2), R(src, t, 1280, 4), 0.5)
 
     def passes(out, win, off, other, pairs, between):
         def fused(t):
-            pick_tt(R(out, t, 1280, 4), R(win, C * t, C * t + C), R(off), other(t), A.add)
-        pick("s", R(pairs, 1, 640, 2), R(win, 960, 1280), R(off))
-        fused(0)
+            pick_tt(R(out, t, 1280, 4), R(win, C * t, C * t + C), R(off, 0, 20), other(t), A.add)
+        act(R(pairs, 1, 640, 2), R(win, 960, 1280), off=R(off, 0, 20))
         between[0]()
-        scan(R(out, 1, 1280, 2), R("z01"), R(pairs), A.mult, A.add)
+        fused(0)
         between[1]()
         fused(2)
+        between[2]()
+        scan(R(out, 1, 1280, 2), R("z01"), R(pairs))
+        between[3]()
         fused(1)
-
-    ts(R("vf"), R("ie", 0, 10), 2.0, A.mult, one("p31f"), A.add)
-    fill(R("fl", 20, 22), 0)
-    ts(R("vf"), R("vf"), 160.0, A.subtract)
-    lists("f", 0, R("vf"), 0, 128, 1)
-    window_list("f", "kw")
-    waiting += [
-        lambda: op("v", [R("qir")], [R("qo16"), R("iot")], lambda: g.vector.tensor_copy(ap(R("qir")).indirect(ap(R("qo16"))), ap(R("iot")))),
-        lambda: unrow("qiw", "qir"),
-        lambda: ts(R("qio"), R("qiw"), 160.0, A.add),
-        lambda: (pick("s", R("mqr"), R("mr"), R("qio")), planes("xt")),
-        lambda: lists("b", 0, R("vf"), 0, 128, 1),
-        lambda: copy(R("ac", 0, 20), R("iwc")),
-        lambda: unrow("mqw", "mqr"),
-        lambda: turn(R("at"), R("ac")),
-        lambda: tables("b", "qiw", "mqw"),
-        lambda: copy(R("a2", 0, 16, 1, 0, 32), R("at", 0, 16, 1, 0, 32)),
-        lambda: window_list("b", "low")]
 
     def nothing():
         pass
+
+    def seq(*fs):
+        return lambda: [f() for f in fs]
+
+    def roles():
+        tables("f", "rt", 0, 320)
+        ts(one("im"), one("g3"), 2.0, A.is_ge, 1.0, A.add)
+        act(R("nn", 1, 320, 8), R("i40"), 1.0, one("fn"))
+        act(one("ic"), one("d"), one("c2"), one("fn"))
+        for k in range(2):
+            act(R("t2", ENTRY + 16 * k, 320, 32), R("ie", 0, 20, 2), one("im"), one("ic"))
+        act(one("c3"), one("p31"), 1.0, one("zo"))
+        act(one("d160"), one("d"), 160.0)
+        act(one("rof"), one("d"), BOTH - FIRST, float(FIRST))
+        act(one("rob"), one("d"), FIRST - BOTH, float(BOTH))
+        act(R("iw"), R("iw"), 1.0, one("r"))
+        planes("xt")
+        turn(R("rt", 960, 1280), R("rw", 960, 1280))
+
+    def mates():
+        for k in range(4):
+            lin(R("nn", 2 + 8 * k, 320, 32, *quad(3)), R("rt", 976, 1280, 32, *quad(3)), 2.0, 0.0)
+
+    def entries():
+        lin(R("l2f"), R("ie", 0, 10), 2.0, one("p31"))
+        ts(R("jn"), R("ie", 0, 2), one("r"), A.add, 19.0, A.min)
+
+    def inverse():
+        lin(R("pl", 6, 8), R("ie", 0, 2), R("m2", 1, 2), R("cA", 1, 2))
+        lin(R("pl", 8, 10), R("ie", 0, 2), R("m2", 1, 2), R("cB", 1, 2))
+        op("v", [R("sc")], [R("qo16"), R("bl")], lambda: g.vector.tensor_copy(ap(R("sc")).indirect(ap(R("qo16"))), ap(R("bl"))))
+
+    def orders():
+        ts(R("lb"), R("iw"), 0.0, A.add, off=R("pl", 6, 10))
+        act(R("rb2", 0, 320), R("sc"), off=R("lb", 0, 20))
+        act(R("rb2", 320, 640), R("sc"), off=R("lb", 32, 52))
+        act(R("w2"), R("z01"), 0.0, 0.5)
+        act(one("mb"), one("d"), 0.0, 0.5)
+        act(one("mb", 3), one("d", 3), 0.0, 0.25)
+
+    def selects():
+        ts(R("l3f"), R("i3"), one("c3"), A.add, 160.0, A.subtract)
+        ts(R("ge"), R("jn"), 10.0, A.is_ge, one("cx"), A.mult)
+        lin(R("j16"), R("jn"), 16.0, one("d160"))
+
+    def selects2():
+        tt(R("base"), R("ge"), R("j16"), A.add)
+        ts(one("c1"), one("r2"), 4.0, A.min, 32.0, A.mult)
+
+    def selects3():
+        ts(R("sef"), R("base"), one("rof"), A.add)
+        ts(one("c2"), one("cx"), 160.0, A.add, one("b0"), A.mult)
+        lin(one("kp"), one("d"), 176.0, one("c1"))
+
+    def selects4():
+        ts(R("al", 0, 2), R("base"), float(FIRST), A.add)
+        ts(R("al", 2, 4), R("base"), float(ENTRY), A.add)
+        ts(R("al", 4, 5), one("kp"), one("c2"), A.add, float(FIRST), A.add)
+        ts(R("al", 5, 6), one("kp"), one("c2"), A.add, float(MATE), A.add)
+
+    def back2():
+        turn(R("tb2"), R("rb2"))
+        ts(one("rs"), one("r2"), 1.0, A.is_equal, 4.0, A.mult)
+        tt(R("km", 0, 20), R("tb2", 320, 640, 16), R("tb2", 321, 640, 16), A.min)
+        tables("b", "tb2", 0, 1)
+        act(one("rz"), one("rs"), -0.5, 2.0)
+        ts(R("kb", 0, 10), R("km", 1, 20, 2), 160.0, A.add)
+        ts(R("krb", 0, 10), R("km", 1, 20, 2), 160.0, A.add)
+        ts(R("kb", 10, 20), R("km", 0, 20, 2), 160.0, A.add)
+        ts(R("krb", 10, 20), R("km", 0, 20, 2), 480.0, A.add)
+
+    later = [lambda: lin(R("l2b"), R("ie", 0, 10), 2.0, one("p31")),
+             lambda: ts(R("l3b"), R("i3"), one("c3"), A.add, 160.0, A.subtract)]
+    later += [lambda b=b: quant("eq", R("et", 512 * b, 512 * b + 512), 128 * b, 128 * b + 128) for b in (0, 3, 2, 1)]
+    later += [
+             lambda: ts(R("seb"), R("base"), one("rob"), A.add),
+             lambda: ts(R("bm", 0, 2), R("base"), float(FIRST), A.add),
+             lambda: ts(R("bm", 2, 4), R("base"), float(BOTH), A.add),
+             lambda: ts(R("krf", 0, 10), R("kf", 0, 10), 320.0, A.add),
+             lambda: copy(R("krf", 10, 20), R("kf", 10, 20)),
+             lambda: (fill(R("tw", 0, 1), 0.5), fill(R("tw", 1, 16), -0.5))]
 
     for rnd, s in enumerate(ROUNDS):
         peer = T.cores[rank ^ s]
         rid, pid, _se = topo.addr(peer)
         mask, neng = topo.mask(core, peer), len(topo.engines(core, peer))
-        choose("f")
-        spare()
-        rows("f")
-        spare()
-        compose("f", spare)
-        turn(R("tt", 0, 320, 1, 0, 32), R("frf", 1104, 1424, 1, 0, 32))
-        spare()
-        lists("f", 1, *turned(0, 32), 1)
-        step("f", 1, 2, 1)
-        step("f", 2, 3, 2)
-        finish("f", "xo", (2,))
-        while waiting:
-            spare()
-        passes("vt", "xp", "xo", lambda t: R("xi", C * t, C * t + C), "ys", (nothing, nothing))
+        last = rnd == 2
+        if rnd == 0:
+            chain(rnd, "f", (roles, mates, entries, inverse, orders, selects, selects2, selects3, selects4))
+        else:
+            chain(rnd, "f", (nothing,) * 9)
+
+        def start1():
+            act(R("aa"), R("xf"), off=R("al"))
+            tt(R("km3", 0, 10, 1, *quad(3)), R("xf", FIRST, 160, 16, *quad(3)), R("xf", MATE, 160, 16, *quad(3)), A.min)
+
+        def start2():
+            if rnd == 0:
+                back2()
+            lin(R("krb", 0, 10, 1, *quad(3)), R("km3", 0, 10, 1, *quad(3)), 0.5, 800.0)
+            lin(R("kb", 0, 10, 1, *quad(3)), R("km3", 0, 10, 1, *quad(3)), 0.5, 160.0)
+            act(R("rb"), R("wb"), one("rs"), one("rz"), off=R("krb"))
+
+        def start3():
+            tt(R("e1b", 0, 80, 8, *quad(3)), R("aa", 64, 74, 1, *quad(3)), R("aa", 80, 90, 1, *quad(3)), A.subtract)
+            tt(R("e1b", 1, 80, 8, *quad(3)), R("aa", 64, 74, 1, *quad(3)), R("aa", 80, 90, 1, *quad(3)), A.add)
+        passes("vt", "xp", "xo", lambda t: R("xi", C * t, C * t + C), "ys", (start1, start2, nothing, start3))
         halves("vq", "vt", True)
         for h, (c0, c1) in enumerate(HALVES):
             for b in range(4):
                 k = ring()
                 mx(k, c1 - c0, "wq", 128 * b, "vq", c0)
-                act(R("ht", 4 * c0 + b, 4 * c1, 4), R("ps%d" % k, 0, c1 - c0), F.Copy, scale=0.03125)
-        act(R("yv", 0, 640, 2), R("vt", 3, 1280, 4), F.Copy)
-        pick("v", R("rr8"), R("frf", 1088, 1440), R("sl"))
-        ts(R("ac", 0, 20), R("xo"), 160.0, A.subtract)
-        turn(R("tt", 0, 160, 1, 96, 128), R("rr8", 0, 160, 1, 96, 128))
-        turn(R("at"), R("ac"))
-        lists("b", 3, *turned(3, 16), 1)
+                act(R("ht", 4 * c0 + b, 4 * c1, 4), R("ps%d" % k, 0, c1 - c0), 0.03125)
+        act(R("yv", 0, 640, 2), R("vt", 3, 1280, 4))
         if rnd == 0:
             quant("vvq", R("vv"), 0, 128)
-        waiting.append(lambda: copy(R("a2", 16, 32), R("at", 0, 16)))
-        waiting += [lambda q=q: copy(R("a2", 0, 16, 1, 32 * q + 32, 32 * q + 64), R("at", 16, 32, 1, 32 * q, 32 * q + 32)) for q in range(3)]
+            waiting += later
+        signs("sgb", 0)
+        signs("sgb", 1)
 
         def send(h):
             c0, c1 = C * rnd + HALVES[h][0], C * rnd + HALVES[h][1]
@@ -414,53 +479,55 @@ def rank_program(g, core, T, topo):
             clock[(sem, 2 * neng)] = {}
             note([R("rqc", c0, c1), R("rqs", c0, c1)], [], (sem, 2 * neng))
 
-        choose("b")
-        spare()
-        rows("b")
-        send(0)
-        compose("b", lambda: send(1))
-        step("b", 3, 2, 1)
-        step("b", 2, 1, 1)
-        if rnd == 0:
-            quant("eq", R("et"), 0, 512)
-        step("b", 1, 0, 0)
-        for h, (c0, c1) in enumerate(HALVES):
-            for b in range(4):
-                k = ring()
-                mx(k, c1 - c0, "eq", 128 * b, "rq", C * rnd + c0)
-                act(R("dp", C * b + c0, C * b + c1), R("ps%d" % k, 0, c1 - c0), F.Copy)
-        finish("b", "xob", (1, 3))
-        while waiting:
-            spare()
-        xn = "xn%d" % rnd
-        last = rnd == 2
+        def unpack():
+            for h, (c0, c1) in enumerate(HALVES):
+                for b in (0, 3, 2, 1):
+                    k = ring()
+                    mx(k, c1 - c0, "eq", 128 * b, "rq", C * rnd + c0)
+                    act(R("dp", C * b + c0, C * b + c1), R("ps%d" % k, 0, c1 - c0))
 
-        def misses():
-            cu, old = "cu%d" % (rnd % 2), "cu%d" % (1 - rnd % 2)
-            tt(R("md" if rnd else cu), R("a2"), R("bt"), A.not_equal)
+        chain(rnd, "b", (spare, lambda: send(0), spare, seq(lambda: send(1), lambda: spare(2)), lambda: spare(2), seq(lambda: spare(2), unpack),
+                         spare, lambda: spare(2), lambda: spare(2)))
+        xn = "xn%d" % rnd
+        cu, old = "cu%d" % (rnd % 2), "cu%d" % (1 - rnd % 2)
+
+        def miss1():
+            pick_tt(R("md" if rnd else cu), R("xb"), R("bm"), R("aa", 0, 64), A.not_equal)
+
+        def miss2():
             if rnd:
                 tt(R(cu), R(old), R("md"), A.not_equal)
-            turn(R("cut"), R(cu))
-            copy(R("moff"), R("cut"))
-            a, b = (320, 0) if last else (0, 320)
-            pick("s", R("w", a, a + 320), R("tw2"), R("moff", 0, 20))
-            act(R("w", b, b + 320), R("w", a, a + 320), F.Copy, scale=-1.0)
-            pick("s", R("d1f", 0, 640, 2) if last else R("tf"), R("w"), R("ktf"))
-        ts(R("bc", 0, 20), R("xob"), 160.0, A.subtract)
-        passes(xn, "dp", "xob", lambda t: R("vt", t, 1280, 4), "yv", (lambda: turn(R("bt"), R("bc")), misses))
+
+        def miss3():
+            copy(R("moff"), R(cu))
+            act(R("w2", 0, 320), R("tw"), off=R("moff", 0, 20))
+            act(R("w2", 320, 640), R("tw"), off=R("moff", 32, 52))
+            if last:
+                act(R("q0", 2, 960, 3), R("w2"), -1.0, 0.5, off=R("kn"))
+            else:
+                act(R("rf"), R("w2"), one("rs"), one("rz"), off=R("krf"))
+        passes(xn, "dp", "xob", lambda t: R("vt", t, 1280, 4), "yv", (miss1, miss2, miss3, nothing))
         halves("xq", xn, not last)
         if not last:
             planes(xn)
-            pick("s", R("tb"), R("w"), R("ktb"))
+            signs("sgf", 0)
+            signs("sgf", 1)
+        if rnd == 1:
+            act(R("q1", 0, 960, 3), R("qr"), off=R("mo16"))
+            act(R("q1", 1, 960, 3), R("qr"), -1.0)
+            act(R("q1", 2, 960, 3), R("qr"))
+            act(one("kp"), one("d"), -320.0, 320.0)
+            waiting.append(lambda: ts(R("kn"), R("gg", 64, 84), one("kp"), A.add))
 
+    dma("y", [], [R("xqc")], T.oc[:, :], T.xqc[:, :].bitcast(dt.uint8))
     for h, (c0, c1) in enumerate(HALVES):
         mx(h, c1 - c0, "vvq", 0, "xq", c0)
+    scan(R("q2"), R("q0"), R("q1"))
+    act(R("qout"), R("q2", 2, 960, 3), 1.0, 160.0)
+    dma("s", [], [R("qout")], T.qo[:, :], T.qout[0:128:16, :])
+    for h, (c0, c1) in enumerate(HALVES):
         copy(R("yt", c0, c1), R("ps%d" % h, 0, c1 - c0))
         dma("y", [], [R("yt", c0, c1)], T.y[:, c0:c1], ap(R("yt", c0, c1)))
-    rows("f")
-    act(R("qout"), R("frf", 65, 704, 2), F.Identity, bias=160.0)
-    dma("s", [], [R("qout")], T.qo[:, :], T.qout[0:128:16, :])
-    dma("y", [], [R("xqc")], T.oc[:, :], T.xqc[:, :].bitcast(dt.uint8))
     for k in range(4):
         dma("y", [], [R("xqs")], T.osc[4 * k:4 * k + 4, :], T.xqs[32 * k:32 * k + 4, :])
     for sem, val in sorted(pending.items()):

@@ -13,14 +13,14 @@ def _buf(dtype, **widths):
         SCRATCH[k] = ("sbuf", [128, n], dtype)
 
 
-_buf("bfloat16", xt=1280, xn0=1280, xn1=1280, xn2=1280, xp=1280, vt=1280, ht=1280, dp=1280, ut=512, vv=512, et=2048, ones=512,
-     iot=320, xi=960, tw=16, z01=640, ys=640, yv=640, qr=320, rw=1280, rt=1280, bl=320, sc=320, rb2=640, tb2=640,
+_buf("bfloat16", xt=1280, xn0=1280, xn1=1280, xn2=1280, xp=1280, xi=640, vt=1280, ht=1280, dp=1280, ut=512, vv=512, et=2048, ones=512,
+     iot=320, tw=16, ys=640, qr=320, rw=1280, rt=1280, bl=320, sc=320, rb2=640, tb2=640,
      wb=960, sgb=320, rf=320, rb=320, pk=320, t0=320, m1=80, nn=320, nw=320, g1=160, t2=320, gw=320, zw=480, t3=192, fr=192, xf=352, xb=352,
      aa=96, md=64, cu0=64, cu1=64, km=30, q0=960, q1=960, q2=960)
 _buf("float32", col=32, fb=8, sm=48, ie=20, iw=96, i40=40, ef=160, eb=160, qout=320, yt=320)
 _buf("int32", ib=8, gg=96, iwi=20)
-_buf("uint16", offu=8, qo16=20, mo16=20, pl=10, la=96, lb=64, kf=20, kb=20, krf=20, krb=20, kn=20, l1=10, l2f=10, l2b=10, l3f=10, l3b=10,
-     sef=2, seb=2, al=6, bm=4, xo=32, xob=32, moff=64)
+_buf("uint16", offu=8, qo16=20, mo16=20, pl=10, la=96, lb=64, kf=20, kb=20, krb=10, kn=20, l1=10, l2f=10, l2b=10, l3f=10, l3b=10,
+     sef=2, seb=2, al=6, bm=4, own=2, xo=32, xob=32, moff=64)
 for _n, _w in (("uq", 128), ("us", 128), ("xq", 320), ("vq", 320), ("vvq", 128), ("eq", 512), ("wq", 512), ("hq", 960), ("rq", 960)):
     SCRATCH[_n + "c"] = ("sbuf", [128, _w], "float8_e4m3fn_x4")
     SCRATCH[_n + "s"] = ("sbuf", [128, _w], "uint8")
@@ -31,10 +31,10 @@ NDMA = 20
 SEMAPHORES = ["qv", "qs", "qt", "qg", "lsem"] + ["d%d" % i for i in range(NDMA)] + ["ar%d_%d" % (r, h) for r in range(3) for h in range(2)]
 
 PLACE = {n: ("fb", i, 1) for i, n in enumerate(("b0", "b0x", "b1", "r", "r2", "r4", "d", "g3"))}
-PLACE.update({n: ("col", i, 1) for i, n in enumerate(("thr", "cs", "rs", "rz", "dl", "xa", "xc", "rd", "p31", "zo", "u16", "lowe", "lowo", "cx", "d160",
-                                                      "rof", "rob", "mb", "fn", "im", "ic", "c1", "c2", "c3", "kp"))})
+PLACE.update({n: ("col", i, 1) for i, n in enumerate(("thr", "cs", "rs", "rz", "dl", "xa", "xc", "rd", "p31", "zo", "u16", "cx", "d160",
+                                                      "rof", "rob", "mb", "fn", "im", "ic", "c1", "c2", "c3", "c4", "c5", "c6", "kp"))})
 PLACE.update({n: ("sm", 2 * i, 2) for i, n in enumerate(("cS", "cH", "fS", "fH", "t1", "cA", "cB", "m2", "jn", "ge", "j16", "base"))})
-PLACE.update({"i3": ("sm", 24, 10), "w2": ("wb", 0, 640), "sgf": ("wb", 640, 320), "km3": ("km", 20, 10),
+PLACE.update({"i3": ("sm", 24, 10), "wo": ("wb", 0, 320), "we": ("wb", 320, 320), "sgf": ("wb", 640, 320), "km3": ("km", 20, 10),
               "e1f": ("ef", 0, 80), "e2f": ("ef", 80, 80), "e1b": ("eb", 0, 80), "e2b": ("eb", 80, 80)})
 ENTRY, FIRST, MATE, BOTH = 1, 2, 4, 8
 
@@ -179,13 +179,6 @@ def rank_program(g, core, T, topo):
     def one(n, q=None):
         return R(n, 0, 1) if q is None else R(n, 0, 1, 1, *quad(q))
 
-    waiting = []
-
-    def spare(n=1):
-        for _ in range(n):
-            if waiting:
-                waiting.pop(0)()
-
     dma("y", [R("gg", 0, 20)], [], ap(R("gg", 0, 20)), T.gq[:, :])
     dma("y", [R("gg", 32, 52)], [], ap(R("gg", 32, 52)), T.gm[:, :])
     dma("y", [R("xt")], [], ap(R("xt")), T.x[:, :])
@@ -206,12 +199,13 @@ def rank_program(g, core, T, topo):
     iota(R("t2"), [[0, 320]], 0)
     iota(R("i3"), [[32, 5], [160, 2]], 0)
     iota(R("bl"), [[1, C]], -160)
+    iota(R("iw"), [[0, 3], [16, 32]], 0)
     for n in ("t3", "fr"):
         iota(R(n), [[0, 192]], 0)
-    iota(R("iw"), [[0, 3], [16, 32]], 0)
     iota(R("eb"), [[0, 160]], 0)
-    iota(R("z01"), [[0, 320], [1, 2]], 0)
     iota(R("ones"), [[0, 512]], 1)
+    for n in ("wo", "we"):
+        op("g", [R(n)], [R("ones")], lambda n=n: g.affine_select(ap(R(n)), ap(R("ones", 0, 320)), [[0, 320]], A.is_gt, 0.5, 0, 0))
     for b in range(4):
         o = R("et", 512 * b, 512 * b + 512)
         op("g", [o], [R("ones")], lambda o=o, b=b: g.affine_select(ap(o), ap(R("ones")), [[-1, 512]], A.is_equal, 0.0, b, 4))
@@ -229,6 +223,8 @@ def rank_program(g, core, T, topo):
     act(one("zo"), one("d"), -160.0, 320.0)
     act(one("cx"), one("d"), -352.0, 32.0)
     act(one("fn"), one("p31"), 2.0, -320.0)
+    act(one("d160"), one("d"), 160.0)
+    act(one("c3"), one("p31"), 1.0, one("zo"))
     ts(one("dl"), one("b0"), one("b1"), A.subtract)
     ts(one("c1"), one("r4"), -2.0, A.mult)
     ts(R("fS", 0, 4), R("cS", 0, 4), one("g3"), A.is_equal)
@@ -271,199 +267,168 @@ def rank_program(g, core, T, topo):
             if decide:
                 mx(h, c1 - c0, "us", 0, name, c0)
 
-    def tables(d, src, no, yes):
-        for e, h in (("e1" + d, 0 if d == "f" else 16), ("e2" + d, 16 if d == "f" else 0)):
-            tt(R(e, 0, 80, 8), R(src, yes + h, yes + 320 - yes % 16, 32), R(src, no + h, no + 320, 32), A.subtract)
-            tt(R(e, 1, 80, 8), R(src, yes + h, yes + 320 - yes % 16, 32), R(src, no + h, no + 320, 32), A.add)
+    def table(e, h, src, no, yes):
+        tt(R(e, 0, 80, 8), R(src, yes + h, yes + 320 - yes % 16, 32), R(src, no + h, no + 320, 32), A.subtract)
+        tt(R(e, 1, 80, 8), R(src, yes + h, yes + 320 - yes % 16, 32), R(src, no + h, no + 320, 32), A.add)
 
     halves("xq", "xt", True)
     pick(R("rw", 320, 640), R("qr"), R("la", 32, 52))
     turn(R("rt", 640, 960), R("rw", 640, 960))
     ts(one("cs"), one("r2"), 1.0, A.min, 0.5, A.mult)
-    ts(one("c2"), one("g3"), 2.0, A.is_lt, 288.0, A.mult)
+    ts(one("im"), one("g3"), 2.0, A.is_ge, 1.0, A.add)
     ts(R("kf", 0, 10), R("rt", 640, 960, 32), 160.0, A.add)
     ts(R("kf", 10, 20), R("rt", 656, 960, 32), 160.0, A.add)
     signs("sgf", 0)
     signs("sgf", 1)
-    turn(R("rt", 0, 640), R("rw", 0, 640))
+    turn(R("rt", 960, 1280), R("rw", 960, 1280))
+    act(R("nn", 1, 320, 8), R("i40"), 1.0, one("fn"))
+    act(one("c2"), one("im"), -288.0, 576.0)
+    for k in range(4):
+        act(R("nn", 2 + 8 * k, 320, 32, *quad(3)), R("rt", 976, 1280, 32, *quad(3)), 2.0)
+    act(one("ic"), one("d"), one("c2"), one("fn"))
+    for k in range(2):
+        act(R("t2", ENTRY + 16 * k, 320, 32), R("ie", 0, 20, 2), one("im"), one("ic"))
+    act(R("iw"), R("iw"), 1.0, one("r"))
 
     def ring():
         state["bank"] += 1
         return 2 + state["bank"] % 6
 
-    def chain(rnd, d, between):
+    def chain(rnd, d, gaps):
+        def gap(k):
+            for f in gaps.get(k, ()):
+                f()
         first, hops, src, to = (0, ((0, 1), (2, 3)), 1, (2, 3)) if d == "f" else (1, ((3, 2), (1, 0)), 2, (1, 0))
-        if d == "f" and rnd == 0:
-            lin(R("pk"), R("sgf"), 2.0, 0.0, off=R("kf"))
-        else:
-            pick_tt(R("pk"), R("sg" + d), R("k" + d), R("r" + d), A.mult)
-        between[0]()
-        turn(R("t0"), R("pk"))
-        between[1]()
+        for c0, c1 in reversed(HALVES):
+            if d == "f" and rnd == 0:
+                lin(R("pk", c0, c1), R("sgf"), 2.0, 0.0, off=R("kf", c0 // 16, c1 // 16))
+            else:
+                pick_tt(R("pk", c0, c1), R("sg" + d), R("k" + d, c0 // 16, c1 // 16), R("r" + d, c0, c1), A.mult)
+        gap(0)
+        for c0, c1 in reversed(HALVES):
+            turn(R("t0", c0, c1), R("pk", c0, c1))
+        gap(1)
         scan(R("nn", 0, 320, 4), R("t0", 161 - first, 320, 2), R("e2" + d))
         scan(R("m1"), R("t0", first, 160, 2), R("e1" + d))
+        gap(2)
         turn(R("nw"), R("nn"))
         lin(R("l1"), R("m1", 1, 80, 8), 0.5 if d == "f" else one("mb"), 160.0)
-        between[2]()
+        gap(3)
         pick(R("g1"), R("nw"), R("l1"))
-        between[3]()
+        gap(4)
         turn(R("t2", 0, 320, 2), R("g1"))
-        between[4]()
+        gap(5)
         turn(R("gw"), R("t2"))
         for a, b in hops:
             lin(R("l2" + d, 0, 10, 1, *quad(b)), R("t2", BOTH, 320, 32, *quad(a)), 0.5, 160.0)
+        gap(6)
         pick(R("zw", 160, 320), R("gw"), R("l2" + d))
-        between[5]()
+        gap(7)
         turn(R("t3", 16, 176), R("zw", 160, 320))
-        between[6]()
+        gap(8)
         turn(R("zw", 0, 160), R("t3", 0, 160))
         turn(R("zw", 320, 480), R("t3", 32, 192))
         for b in to:
             lin(R("l3" + d, 0, 10, 1, *quad(b)), R("t3", 16 + BOTH, 176, 16, *quad(src)), 0.5, one("zo", src))
+        gap(9)
         pick(R("fr", 16, 176), R("zw"), R("l3" + d))
-        between[7]()
+        gap(10)
         turn(R("x" + d, 0, 160), R("fr", 16, 176))
         turn(R("x" + d, 160, 352), R("fr"))
-        between[8]()
+        gap(11)
         lin(R("xo" if d == "f" else "xob"), R("x" + d), 0.5, 160.0, off=R("se" + d))
 
     def planes(src):
         for t in range(4):
             act(R("xp", C * t, C * t + C), R(src, t, 1280, 4), 0.5)
-            act(R("xi", C * t, C * t + C) if t < 3 else R("ys", 0, 640, 2), R(src, t, 1280, 4), 0.5)
+        for t in range(2):
+            act(R("xi", C * t, C * t + C), R(src, t, 1280, 4), 0.5)
 
-    def passes(out, win, off, other, pairs, between):
-        def fused(t):
-            pick_tt(R(out, t, 1280, 4), R(win, C * t, C * t + C), R(off, 0, 20), other(t), A.add)
-        act(R(pairs, 1, 640, 2), R(win, 960, 1280), off=R(off, 0, 20))
-        between[0]()
-        fused(0)
-        between[1]()
-        fused(2)
-        between[2]()
-        scan(R(out, 1, 1280, 2), R("z01"), R(pairs))
-        between[3]()
-        fused(1)
-
-    def nothing():
-        pass
-
-    def seq(*fs):
-        return lambda: [f() for f in fs]
-
-    def roles():
-        tables("f", "rt", 0, 320)
-        ts(one("im"), one("g3"), 2.0, A.is_ge, 1.0, A.add)
-        act(R("nn", 1, 320, 8), R("i40"), 1.0, one("fn"))
-        act(one("ic"), one("d"), one("c2"), one("fn"))
-        for k in range(2):
-            act(R("t2", ENTRY + 16 * k, 320, 32), R("ie", 0, 20, 2), one("im"), one("ic"))
-        act(one("c3"), one("p31"), 1.0, one("zo"))
-        act(one("d160"), one("d"), 160.0)
-        act(one("rof"), one("d"), BOTH - FIRST, float(FIRST))
-        act(one("rob"), one("d"), FIRST - BOTH, float(BOTH))
-        act(R("iw"), R("iw"), 1.0, one("r"))
-        planes("xt")
-        turn(R("rt", 960, 1280), R("rw", 960, 1280))
-
-    def mates():
-        for k in range(4):
-            lin(R("nn", 2 + 8 * k, 320, 32, *quad(3)), R("rt", 976, 1280, 32, *quad(3)), 2.0, 0.0)
-
-    def entries():
-        lin(R("l2f"), R("ie", 0, 10), 2.0, one("p31"))
-        ts(R("jn"), R("ie", 0, 2), one("r"), A.add, 19.0, A.min)
+    def passes(out, win, off, other, aside, gaps):
+        def gap(k):
+            for f in gaps.get(k, ()):
+                f()
+        for i, t in enumerate(aside):
+            act(R("ys", C * i, C * i + C), R(win, C * t, C * t + C), off=R(off, 0, 20))
+        gap(0)
+        for t in range(4 - len(aside)):
+            pick_tt(R(out, t, 1280, 4), R(win, C * t, C * t + C), R(off, 0, 20), other(t, 0, C), A.add)
+            gap(1 + t)
+        for i, t in enumerate(aside):
+            for c0, c1 in HALVES if t == aside[-1] else ((0, C),):
+                tt(R(out, 4 * c0 + t, 4 * c1, 4), R("ys", C * i + c0, C * i + c1), other(t, c0, c1), A.add)
 
     def inverse():
-        lin(R("pl", 6, 8), R("ie", 0, 2), R("m2", 1, 2), R("cA", 1, 2))
-        lin(R("pl", 8, 10), R("ie", 0, 2), R("m2", 1, 2), R("cB", 1, 2))
         op("v", [R("sc")], [R("qo16"), R("bl")], lambda: g.vector.tensor_copy(ap(R("sc")).indirect(ap(R("qo16"))), ap(R("bl"))))
 
     def orders():
         ts(R("lb"), R("iw"), 0.0, A.add, off=R("pl", 6, 10))
-        act(R("rb2", 0, 320), R("sc"), off=R("lb", 0, 20))
         act(R("rb2", 320, 640), R("sc"), off=R("lb", 32, 52))
-        act(R("w2"), R("z01"), 0.0, 0.5)
+        act(R("rb2", 0, 320), R("sc"), off=R("lb", 0, 20))
+        act(one("rof"), one("d"), float(BOTH - FIRST), float(FIRST))
+        act(one("rob"), one("d"), float(FIRST - BOTH), float(BOTH))
         act(one("mb"), one("d"), 0.0, 0.5)
         act(one("mb", 3), one("d", 3), 0.0, 0.25)
+        act(one("c6"), one("d"), -32.0, 32.0)
 
-    def selects():
-        ts(R("l3f"), R("i3"), one("c3"), A.add, 160.0, A.subtract)
-        ts(R("ge"), R("jn"), 10.0, A.is_ge, one("cx"), A.mult)
-        lin(R("j16"), R("jn"), 16.0, one("d160"))
-
-    def selects2():
-        tt(R("base"), R("ge"), R("j16"), A.add)
-        ts(one("c1"), one("r2"), 4.0, A.min, 32.0, A.mult)
-
-    def selects3():
-        ts(R("sef"), R("base"), one("rof"), A.add)
-        ts(one("c2"), one("cx"), 160.0, A.add, one("b0"), A.mult)
-        lin(one("kp"), one("d"), 176.0, one("c1"))
-
-    def selects4():
-        ts(R("al", 0, 2), R("base"), float(FIRST), A.add)
-        ts(R("al", 2, 4), R("base"), float(ENTRY), A.add)
-        ts(R("al", 4, 5), one("kp"), one("c2"), A.add, float(FIRST), A.add)
-        ts(R("al", 5, 6), one("kp"), one("c2"), A.add, float(MATE), A.add)
-
-    def back2():
-        turn(R("tb2"), R("rb2"))
-        ts(one("rs"), one("r2"), 1.0, A.is_equal, 4.0, A.mult)
-        tt(R("km", 0, 20), R("tb2", 320, 640, 16), R("tb2", 321, 640, 16), A.min)
-        tables("b", "tb2", 0, 1)
-        act(one("rz"), one("rs"), -0.5, 2.0)
-        ts(R("kb", 0, 10), R("km", 1, 20, 2), 160.0, A.add)
-        ts(R("krb", 0, 10), R("km", 1, 20, 2), 160.0, A.add)
-        ts(R("kb", 10, 20), R("km", 0, 20, 2), 160.0, A.add)
-        ts(R("krb", 10, 20), R("km", 0, 20, 2), 480.0, A.add)
-
-    later = [lambda: lin(R("l2b"), R("ie", 0, 10), 2.0, one("p31")),
-             lambda: ts(R("l3b"), R("i3"), one("c3"), A.add, 160.0, A.subtract)]
-    later += [lambda b=b: quant("eq", R("et", 512 * b, 512 * b + 512), 128 * b, 128 * b + 128) for b in (0, 3, 2, 1)]
-    later += [
-             lambda: ts(R("seb"), R("base"), one("rob"), A.add),
-             lambda: ts(R("bm", 0, 2), R("base"), float(FIRST), A.add),
-             lambda: ts(R("bm", 2, 4), R("base"), float(BOTH), A.add),
-             lambda: ts(R("krf", 0, 10), R("kf", 0, 10), 320.0, A.add),
-             lambda: copy(R("krf", 10, 20), R("kf", 10, 20)),
-             lambda: (fill(R("tw", 0, 1), 0.5), fill(R("tw", 1, 16), -0.5))]
+    first_out = {
+        0: [lambda: turn(R("rt", 0, 640), R("rw", 0, 640))],
+        1: [lambda: table("e2f", 16, "rt", 0, 320), lambda: table("e1f", 0, "rt", 0, 320), lambda: planes("xt")],
+        2: [lambda: lin(R("l2f"), R("ie", 0, 10), 2.0, one("p31"))],
+        3: [lambda: lin(R("pl", 6, 8), R("ie", 0, 2), R("m2", 1, 2), R("cA", 1, 2)), lambda: lin(R("pl", 8, 10), R("ie", 0, 2), R("m2", 1, 2), R("cB", 1, 2))],
+        4: [inverse],
+        5: [orders],
+        6: [lambda: ts(R("jn"), R("ie", 0, 2), one("r"), A.add, 19.0, A.min), lambda: ts(R("l3f"), R("i3"), one("c3"), A.add, 160.0, A.subtract)],
+        7: [lambda: ts(R("ge"), R("jn"), 10.0, A.is_ge, one("cx"), A.mult), lambda: lin(R("j16"), R("jn"), 16.0, one("d160"))],
+        8: [lambda: tt(R("base"), R("ge"), R("j16"), A.add), lambda: ts(one("c4"), one("r2"), 4.0, A.min, 32.0, A.mult)],
+        9: [lambda: ts(R("sef"), R("base"), one("rof"), A.add), lambda: ts(one("c5"), one("cx"), 160.0, A.add, one("b0"), A.mult)],
+        10: [lambda: lin(one("kp"), one("d"), 176.0, one("c4")), lambda: ts(R("al", 0, 2), R("base"), float(FIRST), A.add),
+             lambda: ts(R("al", 2, 4), R("base"), float(ENTRY), A.add)],
+        11: [lambda: ts(R("al", 4, 5), one("kp"), one("c5"), A.add, float(FIRST), A.add), lambda: ts(R("al", 5, 6), one("kp"), one("c5"), A.add, float(MATE), A.add)]}
+    back_lists = [lambda: turn(R("tb2", 320, 640), R("rb2", 320, 640)), lambda: ts(one("rs"), one("r2"), 1.0, A.is_equal, 4.0, A.mult),
+                  lambda: turn(R("tb2", 0, 320), R("rb2", 0, 320)),
+                  lambda: tt(R("km", 0, 20), R("tb2", 320, 640, 16), R("tb2", 321, 640, 16), A.min), lambda: act(one("rz"), one("rs"), -0.5, 2.0),
+                  lambda: table("e1b", 16, "tb2", 0, 1),
+                  lambda: ts(R("krb"), R("km", 1, 20, 2), 160.0, A.add), lambda: ts(R("kb", 0, 10), R("km", 1, 20, 2), 160.0, A.add),
+                  lambda: ts(R("kb", 10, 20), R("km", 0, 20, 2), 160.0, A.add)]
+    unit = [lambda b=b: quant("eq", R("et", 512 * b, 512 * b + 512), 128 * b, 128 * b + 128) for b in (3, 2, 0, 1)]
+    first_back = {0: [lambda: lin(R("l2b"), R("ie", 0, 10), 2.0, one("p31"))], 1: [], 2: [],
+                  3: unit[0:1], 4: [], 5: unit[1:2], 6: unit[2:4],
+                  7: [lambda: ts(R("l3b"), R("i3"), one("c3"), A.add, 160.0, A.subtract), lambda: ts(R("seb"), R("base"), one("rob"), A.add)],
+                  8: [lambda: ts(R("bm", 0, 2), R("base"), float(FIRST), A.add), lambda: ts(R("bm", 2, 4), R("base"), float(BOTH), A.add)],
+                  9: [lambda: fill(R("tw", 0, 1), 0.5), lambda: fill(R("tw", 1, 16), -0.5)]}
 
     for rnd, s in enumerate(ROUNDS):
         peer = T.cores[rank ^ s]
         rid, pid, _se = topo.addr(peer)
         mask, neng = topo.mask(core, peer), len(topo.engines(core, peer))
         last = rnd == 2
-        if rnd == 0:
-            chain(rnd, "f", (roles, mates, entries, inverse, orders, selects, selects2, selects3, selects4))
-        else:
-            chain(rnd, "f", (nothing,) * 9)
+        chain(rnd, "f", first_out if rnd == 0 else {})
 
         def start1():
             act(R("aa"), R("xf"), off=R("al"))
             tt(R("km3", 0, 10, 1, *quad(3)), R("xf", FIRST, 160, 16, *quad(3)), R("xf", MATE, 160, 16, *quad(3)), A.min)
 
         def start2():
-            if rnd == 0:
-                back2()
             lin(R("krb", 0, 10, 1, *quad(3)), R("km3", 0, 10, 1, *quad(3)), 0.5, 800.0)
-            lin(R("kb", 0, 10, 1, *quad(3)), R("km3", 0, 10, 1, *quad(3)), 0.5, 160.0)
-            act(R("rb"), R("wb"), one("rs"), one("rz"), off=R("krb"))
+            act(R("rb", 0, 160), R("wb"), one("rs"), one("rz"), off=R("krb"))
+            act(R("rb", 160, 320), R("we"), one("rs"), one("rz"), off=R("kb", 10, 20))
 
         def start3():
+            lin(R("kb", 0, 10, 1, *quad(3)), R("km3", 0, 10, 1, *quad(3)), 0.5, 160.0)
             tt(R("e1b", 0, 80, 8, *quad(3)), R("aa", 64, 74, 1, *quad(3)), R("aa", 80, 90, 1, *quad(3)), A.subtract)
             tt(R("e1b", 1, 80, 8, *quad(3)), R("aa", 64, 74, 1, *quad(3)), R("aa", 80, 90, 1, *quad(3)), A.add)
-        passes("vt", "xp", "xo", lambda t: R("xi", C * t, C * t + C), "ys", (start1, start2, nothing, start3))
+        passes("vt", "xp", "xo", lambda t, c0, c1: R("xi" if t < 2 else "xp", C * t + c0, C * t + c1), (3, 2),
+               {0: [start1], 1: (back_lists if rnd == 0 else []) + [start2]})
         halves("vq", "vt", True)
         for h, (c0, c1) in enumerate(HALVES):
             for b in range(4):
                 k = ring()
                 mx(k, c1 - c0, "wq", 128 * b, "vq", c0)
                 act(R("ht", 4 * c0 + b, 4 * c1, 4), R("ps%d" % k, 0, c1 - c0), 0.03125)
-        act(R("yv", 0, 640, 2), R("vt", 3, 1280, 4))
+        start3()
         if rnd == 0:
-            quant("vvq", R("vv"), 0, 128)
-            waiting += later
+            table("e2b", 0, "tb2", 0, 1)
         signs("sgb", 0)
         signs("sgb", 1)
 
@@ -481,13 +446,17 @@ def rank_program(g, core, T, topo):
 
         def unpack():
             for h, (c0, c1) in enumerate(HALVES):
-                for b in (0, 3, 2, 1):
+                for b in (0, 3, 1, 2):
                     k = ring()
                     mx(k, c1 - c0, "eq", 128 * b, "rq", C * rnd + c0)
                     act(R("dp", C * b + c0, C * b + c1), R("ps%d" % k, 0, c1 - c0))
 
-        chain(rnd, "b", (spare, lambda: send(0), spare, seq(lambda: send(1), lambda: spare(2)), lambda: spare(2), seq(lambda: spare(2), unpack),
-                         spare, lambda: spare(2), lambda: spare(2)))
+        gaps = {k: list(v) for k, v in first_back.items()} if rnd == 0 else {}
+        if last:
+            gaps = {5: [lambda: quant("vvq", R("vv"), 0, 128)], 6: [lambda: copy(R("kn"), R("gg", 64, 84)), lambda: ts(R("own"), R("jn"), one("c6"), A.add)]}
+        for k, f in ((1, lambda: send(0)), (4, lambda: send(1)), (7, unpack)):
+            gaps.setdefault(k, []).append(f)
+        chain(rnd, "b", gaps)
         xn = "xn%d" % rnd
         cu, old = "cu%d" % (rnd % 2), "cu%d" % (1 - rnd % 2)
 
@@ -499,14 +468,16 @@ def rank_program(g, core, T, topo):
                 tt(R(cu), R(old), R("md"), A.not_equal)
 
         def miss3():
-            copy(R("moff"), R(cu))
-            act(R("w2", 0, 320), R("tw"), off=R("moff", 0, 20))
-            act(R("w2", 320, 640), R("tw"), off=R("moff", 32, 52))
             if last:
-                act(R("q0", 2, 960, 3), R("w2"), -1.0, 0.5, off=R("kn"))
-            else:
-                act(R("rf"), R("w2"), one("rs"), one("rz"), off=R("krf"))
-        passes(xn, "dp", "xob", lambda t: R("vt", t, 1280, 4), "yv", (miss1, miss2, miss3, nothing))
+                ts(R("moff", 0, 32), R(cu), 0.0, A.add, off=R("own"))
+                act(R("wo"), R("tw"), off=R("moff", 0, 20))
+                act(R("q0", 2, 960, 3), R("wo"), -1.0, 0.5, off=R("kn"))
+                return
+            copy(R("moff"), R(cu))
+            for w, at, c0 in (("wo", 0, 160), ("we", 32, 0)):
+                act(R(w), R("tw"), off=R("moff", at, at + 20))
+                act(R("rf", c0, c0 + 160), R(w), one("rs"), one("rz"), off=R("kf", c0 // 16, c0 // 16 + 10))
+        passes(xn, "dp", "xob", lambda t, c0, c1: R("vt", 4 * c0 + t, 4 * c1, 4), (3,), {0: [miss1], 1: [miss2], 2: [miss3]})
         halves("xq", xn, not last)
         if not last:
             planes(xn)
@@ -516,20 +487,17 @@ def rank_program(g, core, T, topo):
             act(R("q1", 0, 960, 3), R("qr"), off=R("mo16"))
             act(R("q1", 1, 960, 3), R("qr"), -1.0)
             act(R("q1", 2, 960, 3), R("qr"))
-            act(one("kp"), one("d"), -320.0, 320.0)
-            waiting.append(lambda: ts(R("kn"), R("gg", 64, 84), one("kp"), A.add))
 
     dma("y", [], [R("xqc")], T.oc[:, :], T.xqc[:, :].bitcast(dt.uint8))
-    for h, (c0, c1) in enumerate(HALVES):
-        mx(h, c1 - c0, "vvq", 0, "xq", c0)
-    scan(R("q2"), R("q0"), R("q1"))
-    act(R("qout"), R("q2", 2, 960, 3), 1.0, 160.0)
-    dma("s", [], [R("qout")], T.qo[:, :], T.qout[0:128:16, :])
-    for h, (c0, c1) in enumerate(HALVES):
-        copy(R("yt", c0, c1), R("ps%d" % h, 0, c1 - c0))
-        dma("y", [], [R("yt", c0, c1)], T.y[:, c0:c1], ap(R("yt", c0, c1)))
     for k in range(4):
         dma("y", [], [R("xqs")], T.osc[4 * k:4 * k + 4, :], T.xqs[32 * k:32 * k + 4, :])
+    for h, (c0, c1) in enumerate(HALVES):
+        mx(h, c1 - c0, "vvq", 0, "xq", c0)
+        act(R("yt", c0, c1), R("ps%d" % h, 0, c1 - c0))
+        dma("y", [], [R("yt", c0, c1)], T.y[:, c0:c1], ap(R("yt", c0, c1)))
+    scan(R("q2"), R("q0"), R("q1"))
+    ts(R("qout"), R("q2", 2, 960, 3), 160.0, A.add)
+    dma("s", [], [R("qout")], T.qo[:, :], T.qout[0:128:16, :])
     for sem, val in sorted(pending.items()):
         g.wait_ge(T.sem[sem], val)
     for sem, val in count.items():

@@ -4,6 +4,7 @@ C = 320
 ROUNDS = (1, 2, 4)
 HALVES = ((0, 160), (160, 320))
 BIG = 1e29
+DEC, SEND, SB = 1, (3, 5), (0, 1)
 
 SCRATCH = {}
 
@@ -14,13 +15,12 @@ def _buf(dtype, **widths):
 
 
 _buf("bfloat16", xt=1280, xn0=1280, xn1=1280, xn2=1280, xp=1280, xi=640, vt=1280, ht=1280, dp=1280, ut=512, vv=512, et=2048, ones=512,
-     iot=320, tw=16, ys=640, qr=320, rw=1280, rt=1280, bl=320, sc=320, rb2=640, tb2=640,
-     wb=960, sgb=320, rf=320, rb=320, pk=320, t0=320, m1=80, nn=320, nw=320, g1=160, t2=320, gw=320, zw=480, t3=192, fr=192, xf=352, xb=352,
+     iot=320, ys=960, qr=320, rw=1280, rt=1280, bl=320, sc=320, rb2=640, tb2=640, wr=320, nr=320, sgf=320, sgb=320, r1f=160, r1b=160, r2f=160, r2b=160,
+     trf=160, trb=160, pk=320, t0=320, m1=80, nn=320, nw=320, g1=160, t2=320, gw=320, zw=480, t3=192, fr=192, xf=352, xb=352,
      aa=96, md=64, cu0=64, cu1=64, km=30, q0=960, q1=960, q2=960)
-_buf("float32", col=32, fb=8, sm=48, ie=20, iw=96, i40=40, ef=160, eb=160, qout=320, yt=320)
-_buf("int32", ib=8, gg=96, iwi=20)
-_buf("uint16", offu=8, qo16=20, mo16=20, pl=10, la=96, lb=64, kf=20, kb=20, krb=10, kn=20, l1=10, l2f=10, l2b=10, l3f=10, l3b=10,
-     sef=2, seb=2, al=6, bm=4, own=2, xo=32, xob=32, moff=64)
+_buf("float32", col=32, fb=7, sm=48, ie=20, iw=32, i40=40, i23=40, st=58, ef=160, eb=160, dif=20, qout=320, yt=320)
+_buf("int32", ib=7, gg=96, iwi=20)
+_buf("uint16", offu=8, qo16=20, mo16=20, pl=6, la=96, lb=64, kf=20, kb=20, kn=20, l1=10, sl=60, xo=32, xob=32)
 for _n, _w in (("uq", 128), ("us", 128), ("xq", 320), ("vq", 320), ("vvq", 128), ("eq", 512), ("wq", 512), ("hq", 960), ("rq", 960)):
     SCRATCH[_n + "c"] = ("sbuf", [128, _w], "float8_e4m3fn_x4")
     SCRATCH[_n + "s"] = ("sbuf", [128, _w], "uint8")
@@ -30,13 +30,17 @@ for _b in range(8):
 NDMA = 20
 SEMAPHORES = ["qv", "qs", "qt", "qg", "lsem"] + ["d%d" % i for i in range(NDMA)] + ["ar%d_%d" % (r, h) for r in range(3) for h in range(2)]
 
-PLACE = {n: ("fb", i, 1) for i, n in enumerate(("b0", "b0x", "b1", "r", "r2", "r4", "d", "g3"))}
-PLACE.update({n: ("col", i, 1) for i, n in enumerate(("thr", "cs", "rs", "rz", "dl", "xa", "xc", "rd", "p31", "zo", "u16", "cx", "d160",
-                                                      "rof", "rob", "mb", "fn", "im", "ic", "c1", "c2", "c3", "c4", "c5", "c6", "kp"))})
-PLACE.update({n: ("sm", 2 * i, 2) for i, n in enumerate(("cS", "cH", "fS", "fH", "t1", "cA", "cB", "m2", "jn", "ge", "j16", "base"))})
-PLACE.update({"i3": ("sm", 24, 10), "wo": ("wb", 0, 320), "we": ("wb", 320, 320), "sgf": ("wb", 640, 320), "km3": ("km", 20, 10),
-              "e1f": ("ef", 0, 80), "e2f": ("ef", 80, 80), "e1b": ("eb", 0, 80), "e2b": ("eb", 80, 80)})
+PLACE = {n: ("fb", i, 1) for i, n in enumerate(("b0", "b0x", "b1", "r", "r2", "d", "g3"))}
+PLACE.update({n: ("col", i, 1) for i, n in enumerate(("thr", "cs", "rs", "rz", "dl", "nd", "xa", "xc", "rd", "p31", "zo", "u16", "rof", "rob", "mb", "fn", "im", "ic",
+                                                      "c1", "c2", "c3", "c4", "c5", "c6", "k1", "k2", "k3", "k4", "k6", "k7", "kp"))})
+PLACE.update({n: ("sm", 2 * i, 2) for i, n in enumerate(("cS", "cH", "fS", "fH", "tA", "tB", "cA", "cB", "m2"))})
+PLACE.update({n: ("sm", 18 + 4 * i, 4) for i, n in enumerate(("jn", "ge", "j16", "base"))})
+PLACE.update({n: ("sl", a, w) for n, a, w in (("l2f", 0, 10), ("l2b", 10, 10), ("l3f", 20, 10), ("l3b", 30, 10), ("plb", 40, 4), ("sef", 44, 2), ("seb", 46, 2),
+                                              ("al", 48, 6), ("bm", 54, 4))})
+PLACE.update({"iu": ("sm", 36, 8), "km3": ("km", 20, 10), "e1f": ("ef", 0, 80), "e2f": ("ef", 80, 80), "e1b": ("eb", 0, 80), "e2b": ("eb", 80, 80),
+              "diff": ("dif", 0, 10), "difb": ("dif", 10, 10)})
 ENTRY, FIRST, MATE, BOTH = 1, 2, 4, 8
+EVEN, ODD = 2, 3
 
 
 def R(name, c0=0, c1=None, st=1, p0=0, p1=128):
@@ -168,8 +172,8 @@ def rank_program(g, core, T, topo):
         o = R("ps%d" % bank, 0, n)
         op("t", [R("ps%d" % bank)], [w, ws, m, ms], lambda: g.tensor.matmul_mx(ap(o), ap(w), ap(ws), ap(m), ap(ms), True, True))
 
-    def act(out, src, scale=1.0, bias=0.0, off=None):
-        func = F.Copy if bias == 0.0 else F.Identity
+    def act(out, src, scale=1.0, bias=0.0, off=None, func=None):
+        func = func or (F.Copy if bias == 0.0 else F.Identity)
         op("s", [out], [src] + cols(scale, bias, off),
            lambda: g.scalar.activation(ap(out), ap(src) if off is None else ap(src).indirect(ap(off)), func, bias=arg(bias), scale=arg(scale)))
 
@@ -178,6 +182,10 @@ def rank_program(g, core, T, topo):
 
     def one(n, q=None):
         return R(n, 0, 1) if q is None else R(n, 0, 1, 1, *quad(q))
+
+    def run(calls):
+        for f in calls:
+            f()
 
     dma("y", [R("gg", 0, 20)], [], ap(R("gg", 0, 20)), T.gq[:, :])
     dma("y", [R("gg", 32, 52)], [], ap(R("gg", 32, 52)), T.gm[:, :])
@@ -191,69 +199,74 @@ def rank_program(g, core, T, topo):
     iota(R("iwi", 0, 2), [[0, 2]], 0, 1)
     iota(R("ie"), [[16, 20]], 0)
     iota(R("sm", 0, 4), [[-2, 2], [-1, 2]], 2)
-    iota(R("sm", 36, 44), [[32, 4], [0, 2]], -16)
+    iota(R("iu"), [[32, 4], [0, 2]], -16)
     iota(R("iot"), [[1, C]], -160)
     iota(R("ef"), [[0, 160]], 0)
     iota(R("i40"), [[64, 10], [0, 4]], 0)
     iota(R("nn"), [[0, 320]], 0)
     iota(R("t2"), [[0, 320]], 0)
-    iota(R("i3"), [[32, 5], [160, 2]], 0)
+    iota(R("iw"), [[16, 32]], 0)
+    iota(R("i23", 0, 20), [[0, 2], [32, 10]], 0)
+    iota(R("i23", 20, 40), [[0, 2], [32, 5], [160, 2]], -160)
     iota(R("bl"), [[1, C]], -160)
-    iota(R("iw"), [[0, 3], [16, 32]], 0)
     for n in ("t3", "fr"):
         iota(R(n), [[0, 192]], 0)
     iota(R("eb"), [[0, 160]], 0)
     iota(R("ones"), [[0, 512]], 1)
-    for n in ("wo", "we"):
-        op("g", [R(n)], [R("ones")], lambda n=n: g.affine_select(ap(R(n)), ap(R("ones", 0, 320)), [[0, 320]], A.is_gt, 0.5, 0, 0))
+    op("g", [R("wr")], [R("ones")], lambda: g.affine_select(ap(R("wr")), ap(R("ones", 0, 320)), [[0, 320]], A.is_gt, 0.5, 0, 0))
     for b in range(4):
         o = R("et", 512 * b, 512 * b + 512)
         op("g", [o], [R("ones")], lambda o=o, b=b: g.affine_select(ap(o), ap(R("ones")), [[-1, 512]], A.is_equal, 0.0, b, 4))
+    iota(R("nr"), [[0, 320]], 0)
     iota(R("q0"), [[0, 320], [1, 3]], 0)
 
     for c0, c1 in ((20, 32), (52, 64), (84, 96)):
         fill(R("gg", c0, c1), 0)
-    for c0, c1, sh, mask in ((0, 2, 0, 1), (2, 3, 1, 1), (3, 4, 0, 15), (4, 5, 1, 7), (5, 6, 2, 3), (6, 7, 4, 1), (7, 8, 4, 3)):
+    for c0, c1, sh, mask in ((0, 2, 0, 1), (2, 3, 1, 1), (3, 4, 0, 15), (4, 5, 1, 7), (5, 6, 4, 1), (6, 7, 4, 3)):
         ts(R("ib", c0, c1), R("iwi", 0, c1 - c0), sh, A.arith_shift_right, mask, A.bitwise_and)
     fill(R("cH", 1, 2), 3.0)
     copy(R("fb"), R("ib"))
+    for n, a, b in (("dl", 0, 2), ("nd", 2, 0), ("c1", 2, 4)):
+        tt(one(n), R("ib", a, a + 1), R("ib", b, b + 1), A.subtract)
+    ts(R("fS", 0, 4), R("cS", 0, 4), one("g3"), A.is_equal)
+    ts(one("rd"), one("r"), one("dl"), A.add)
+    lin(one("xc"), one("b0"), 8.0, one("c1"))
+    lin(one("xa"), one("b1"), 8.0, one("c1"))
+    lin(R("tB"), R("fS"), one("nd"), one("rd"))
+    lin(R("tA"), R("fS"), one("dl"), one("r"))
+    lin(R("m2"), R("fH"), -0.5, 1.0)
+    ts(R("iwi"), R("ie"), one("r"), A.add)
+    lin(R("cB", 0, 1), R("fH", 0, 1), one("xc"), R("tB", 0, 1))
+    lin(R("cA", 0, 1), R("fH", 0, 1), one("xa"), R("tA", 0, 1))
     act(one("u16"), one("b0"), 16.0)
     act(one("thr"), one("r2"), -BIG, BIG)
     act(one("p31"), one("d"), 16.0, one("r"))
+    act(one("c4"), one("r2"), func=F.Sign)
+    act(one("c5"), one("g3"), 1.0, -1.5, func=F.Sign)
     act(one("zo"), one("d"), -160.0, 320.0)
-    act(one("cx"), one("d"), -352.0, 32.0)
+    act(one("c6"), one("r2"), 2.0, one("d"))
     act(one("fn"), one("p31"), 2.0, -320.0)
-    act(one("d160"), one("d"), 160.0)
+    act(one("cs"), one("c4"), 0.5)
+    act(one("im"), one("c5"), 0.5, 1.5)
+    act(one("c2"), one("c5"), -144.0, 144.0)
     act(one("c3"), one("p31"), 1.0, one("zo"))
-    ts(one("dl"), one("b0"), one("b1"), A.subtract)
-    ts(one("c1"), one("r4"), -2.0, A.mult)
-    ts(R("fS", 0, 4), R("cS", 0, 4), one("g3"), A.is_equal)
-    lin(one("xa"), one("b1"), 8.0, one("c1"))
-    lin(one("xc"), one("b0"), 8.0, one("c1"))
-    ts(one("rd"), one("r"), one("dl"), A.add, 64.0, A.add)
-    ts(R("t1"), R("fS"), one("dl"), A.mult)
-    lin(R("cA"), R("fH"), one("xa"), one("r"))
-    lin(R("cB"), R("fH"), one("xc"), one("rd"))
-    lin(R("m2"), R("fH"), -0.5, 1.0)
-    tt(R("cA"), R("cA"), R("t1"), A.add)
-    tt(R("cB"), R("cB"), R("t1"), A.subtract)
     copy(R("qo16"), R("gg", 0, 20))
-    ts(R("iwi"), R("ie"), one("r"), A.add)
-    act(R("qr"), R("iot"), off=R("qo16"))
-    lin(R("pl", 0, 2), R("ie", 0, 2), R("m2", 0, 1), R("cA", 0, 1))
-    lin(R("pl", 4, 6), R("ie", 0, 2), R("m2", 0, 1), R("cB", 0, 1))
+    lin(R("pl", 2, 4), R("ie", 0, 2), R("m2", 0, 1), R("cB", 0, 1))
     tt(R("gg", 64, 84), R("gg", 32, 52), R("iwi"), A.min)
-    ts(R("pl", 2, 4), R("pl", 0, 2), 32.0, A.add)
-    ts(R("offu"), R("sm", 36, 44), one("u16"), A.add)
-    quant("uq", R("ut"), 0, 128)
-
-    ts(R("la"), R("gg"), 0.0, A.add, off=R("pl", 0, 6))
-    lin(R("offu", 0, 2), R("fb", 0, 2), -112.0, 112.0)
+    lin(R("pl", 0, 2), R("ie", 0, 2), R("m2", 0, 1), R("cA", 0, 1))
+    act(R("qr"), R("iot"), off=R("qo16"))
+    ts(R("offu"), R("iu"), one("u16"), A.add)
     copy(R("mo16"), R("gg", 32, 52))
+
+    for k, at in ((2, 2), (0, 0), (1, 0)):
+        ts(R("la", 32 * k, 32 * k + 32), R("gg", 32 * k, 32 * k + 32), 0.0, A.add, off=R("pl", at, at + 2))
+        if k == 2:
+            lin(R("offu", 0, 2), R("fb", 0, 2), -112.0, 112.0)
+            quant("uq", R("ut"), 0, 128)
     act(R("rw", 640, 960), R("iot"), off=R("la", 64, 84))
     op("s", [R("uss")], [R("uqs"), R("offu")], lambda: g.scalar.activation(T.uss[:, 0:128], T.uqs[:, 0:128].indirect(T.offu[:, 0:8]), F.Copy))
-    act(R("rw", 0, 320), R("iot"), off=R("la", 0, 20))
     act(R("rw", 960, 1280), R("iot"), off=R("mo16"))
+    act(R("rw", 0, 320), R("iot"), off=R("la", 0, 20))
     op("v", [R("usc")], [R("uqc"), R("offu")], lambda: g.vector.tensor_copy(T.usc[:, 0:128].bitcast(dt.uint32), T.uqc[:, 0:128].bitcast(dt.uint32).indirect(T.offu[:, 0:8])))
     dma("y", [R("bl")], [R("rw", 960, 1280)], T.bl[1:128:2, :], T.rw[1:128:2, 960:1280])
 
@@ -267,54 +280,56 @@ def rank_program(g, core, T, topo):
             if decide:
                 mx(h, c1 - c0, "us", 0, name, c0)
 
-    def table(e, h, src, no, yes):
-        tt(R(e, 0, 80, 8), R(src, yes + h, yes + 320 - yes % 16, 32), R(src, no + h, no + 320, 32), A.subtract)
-        tt(R(e, 1, 80, 8), R(src, yes + h, yes + 320 - yes % 16, 32), R(src, no + h, no + 320, 32), A.add)
+    def table(out, h, src, no, yes, alu):
+        tt(out, R(src, yes + h, yes + 320 - yes % 16, 32), R(src, no + h, no + 320, 32), alu)
+
+    def tables(e, h, src, no, yes):
+        table(R(e, 0, 80, 8), h, src, no, yes, A.subtract)
+        table(R(e, 1, 80, 8), h, src, no, yes, A.add)
 
     halves("xq", "xt", True)
     pick(R("rw", 320, 640), R("qr"), R("la", 32, 52))
     turn(R("rt", 640, 960), R("rw", 640, 960))
-    ts(one("cs"), one("r2"), 1.0, A.min, 0.5, A.mult)
-    ts(one("im"), one("g3"), 2.0, A.is_ge, 1.0, A.add)
+    signs("sgf", 0)
     ts(R("kf", 0, 10), R("rt", 640, 960, 32), 160.0, A.add)
     ts(R("kf", 10, 20), R("rt", 656, 960, 32), 160.0, A.add)
-    signs("sgf", 0)
+    act(R("nn", 1, 320, 8), R("i40"), 1.0, one("fn"))
     signs("sgf", 1)
     turn(R("rt", 960, 1280), R("rw", 960, 1280))
-    act(R("nn", 1, 320, 8), R("i40"), 1.0, one("fn"))
-    act(one("c2"), one("im"), -288.0, 576.0)
-    for k in range(4):
-        act(R("nn", 2 + 8 * k, 320, 32, *quad(3)), R("rt", 976, 1280, 32, *quad(3)), 2.0)
-    act(one("ic"), one("d"), one("c2"), one("fn"))
-    for k in range(2):
-        act(R("t2", ENTRY + 16 * k, 320, 32), R("ie", 0, 20, 2), one("im"), one("ic"))
-    act(R("iw"), R("iw"), 1.0, one("r"))
 
     def ring():
         state["bank"] += 1
         return 2 + state["bank"] % 6
 
-    def chain(rnd, d, gaps):
+    def both(out, at, win, off, share):
+        if share:
+            act(R(out, at + 96, at + 160), R(win), off=R(off, 6, 10))
+            pick(R(out, at, at + 96), R(win), R(off, 0, 6))
+        else:
+            pick(R(out, at, at + 160), R(win), R(off))
+
+    def decide(d):
+        act(R("pk", 160, 320), R("sg" + d), 2.0, off=R("k" + d, 10, 20))
+
+    def chain(rnd, d, share, gaps):
         def gap(k):
-            for f in gaps.get(k, ()):
-                f()
+            run(gaps.get(k, ()))
         first, hops, src, to = (0, ((0, 1), (2, 3)), 1, (2, 3)) if d == "f" else (1, ((3, 2), (1, 0)), 2, (1, 0))
-        for c0, c1 in reversed(HALVES):
-            if d == "f" and rnd == 0:
-                lin(R("pk", c0, c1), R("sgf"), 2.0, 0.0, off=R("kf", c0 // 16, c1 // 16))
-            else:
-                pick_tt(R("pk", c0, c1), R("sg" + d), R("k" + d, c0 // 16, c1 // 16), R("r" + d, c0, c1), A.mult)
+        if d == "f" and rnd == 0:
+            lin(R("pk", 0, 160), R("sgf"), 2.0, 0.0, off=R("kf", 0, 10))
+        else:
+            pick_tt(R("pk", 0, 160), R("sg" + d), R("k" + d, 0, 10), R("r1" + d), A.mult)
         gap(0)
-        for c0, c1 in reversed(HALVES):
+        for c0, c1 in HALVES:
             turn(R("t0", c0, c1), R("pk", c0, c1))
         gap(1)
-        scan(R("nn", 0, 320, 4), R("t0", 161 - first, 320, 2), R("e2" + d))
         scan(R("m1"), R("t0", first, 160, 2), R("e1" + d))
+        scan(R("nn", 0, 320, 4), R("t0", 161 - first, 320, 2), R("e2" + d))
+        lin(R("l1"), R("m1", 1, 80, 8), 0.5 if d == "f" else one("mb"), 160.0)
         gap(2)
         turn(R("nw"), R("nn"))
-        lin(R("l1"), R("m1", 1, 80, 8), 0.5 if d == "f" else one("mb"), 160.0)
         gap(3)
-        pick(R("g1"), R("nw"), R("l1"))
+        both("g1", 0, "nw", "l1", 0 in share)
         gap(4)
         turn(R("t2", 0, 320, 2), R("g1"))
         gap(5)
@@ -322,7 +337,7 @@ def rank_program(g, core, T, topo):
         for a, b in hops:
             lin(R("l2" + d, 0, 10, 1, *quad(b)), R("t2", BOTH, 320, 32, *quad(a)), 0.5, 160.0)
         gap(6)
-        pick(R("zw", 160, 320), R("gw"), R("l2" + d))
+        both("zw", 160, "gw", "l2" + d, 1 in share)
         gap(7)
         turn(R("t3", 16, 176), R("zw", 160, 320))
         gap(8)
@@ -331,106 +346,144 @@ def rank_program(g, core, T, topo):
         for b in to:
             lin(R("l3" + d, 0, 10, 1, *quad(b)), R("t3", 16 + BOTH, 176, 16, *quad(src)), 0.5, one("zo", src))
         gap(9)
-        pick(R("fr", 16, 176), R("zw"), R("l3" + d))
+        both("fr", 16, "zw", "l3" + d, 2 in share)
         gap(10)
         turn(R("x" + d, 0, 160), R("fr", 16, 176))
         turn(R("x" + d, 160, 352), R("fr"))
         gap(11)
         lin(R("xo" if d == "f" else "xob"), R("x" + d), 0.5, 160.0, off=R("se" + d))
 
-    def planes(src):
-        for t in range(4):
-            act(R("xp", C * t, C * t + C), R(src, t, 1280, 4), 0.5)
-        for t in range(2):
-            act(R("xi", C * t, C * t + C), R(src, t, 1280, 4), 0.5)
+    def planes(src, which):
+        for k in which:
+            t = k % 4
+            n = 160 if k == 5 else C
+            act(R("xp" if k < 4 else "xi", C * t, C * t + n), R(src, t, 4 * n, 4), 0.5)
 
-    def passes(out, win, off, other, aside, gaps):
-        def gap(k):
-            for f in gaps.get(k, ()):
-                f()
-        for i, t in enumerate(aside):
-            act(R("ys", C * i, C * i + C), R(win, C * t, C * t + C), off=R(off, 0, 20))
-        gap(0)
-        for t in range(4 - len(aside)):
-            pick_tt(R(out, t, 1280, 4), R(win, C * t, C * t + C), R(off, 0, 20), other(t, 0, C), A.add)
-            gap(1 + t)
-        for i, t in enumerate(aside):
-            for c0, c1 in HALVES if t == aside[-1] else ((0, C),):
-                tt(R(out, 4 * c0 + t, 4 * c1, 4), R("ys", C * i + c0, C * i + c1), other(t, c0, c1), A.add)
+    maps = [[lambda: act(R("q1", 0, 960, 3), R("qr"), off=R("mo16"))],
+            [lambda: act(R("q1", 1, 960, 3), R("qr"), -1.0), lambda: act(R("q1", 2, 960, 3), R("qr"))]]
 
-    def inverse():
-        op("v", [R("sc")], [R("qo16"), R("bl")], lambda: g.vector.tensor_copy(ap(R("sc")).indirect(ap(R("qo16"))), ap(R("bl"))))
+    def passes(out, win, off, other, fused, aside, gaps):
+        for i, (t, c0, c1) in enumerate(aside):
+            act(R("ys", C * i + c0, C * i + c1), R(win, C * t, C * t + C), off=R(off, c0 // 16, c1 // 16))
+        run(gaps.get(0, ()))
+        for i, (t, c0, c1) in enumerate(fused):
+            pick_tt(R(out, 4 * c0 + t, 4 * c1, 4), R(win, C * t, C * t + C), R(off, c0 // 16, c1 // 16), other(t, c0, c1, True), A.add)
+            run(gaps.get(1 + i, ()))
+        for i, (t, c0, c1) in enumerate(aside):
+            for a, b in HALVES if (c1 - c0 == C and i == 1) or len(aside) == 1 else ((c0, c1),):
+                tt(R(out, 4 * a + t, 4 * b, 4), R("ys", C * i + a, C * i + b), other(t, a, b, False), A.add)
+            run(gaps.get(("add", i), ()))
 
-    def orders():
-        ts(R("lb"), R("iw"), 0.0, A.add, off=R("pl", 6, 10))
-        act(R("rb2", 320, 640), R("sc"), off=R("lb", 32, 52))
-        act(R("rb2", 0, 320), R("sc"), off=R("lb", 0, 20))
+    def exchanged(d):
+        return [lambda: turn(R("tr" + d), R("r2" + d)), lambda: tt(R("e2" + d, 0, 80, 8), R("dif" + d), R("tr" + d, ODD if d == "f" else EVEN, 160, 16), A.mult)]
+
+    def roles():
+        for k in range(4):
+            act(R("nn", 2 + 8 * k, 320, 32, *quad(3)), R("rt", 976, 1280, 32, *quad(3)), 2.0)
+        act(one("ic"), one("d"), one("c2"), one("fn"))
+        act(R("iw"), R("iw"), 1.0, one("r"))
+        for k in range(2):
+            act(R("t2", ENTRY + 16 * k, 320, 32), R("ie", 0, 20, 2), one("im"), one("ic"))
+        act(R("cA", 1, 2), R("fH", 1, 2), one("xa"), R("tA", 1, 2))
+        act(R("cB", 1, 2), R("fH", 1, 2), one("xc"), R("tB", 1, 2))
+        act(R("st", 0, 20), R("i23", 0, 20), 1.0, one("p31"))
+        act(R("st", 20, 40), R("i23", 20, 40), 1.0, one("c3"))
+        act(R("st", 40, 42), R("ie", 0, 2), R("m2", 1, 2), R("cA", 1, 2))
+        act(R("st", 42, 44), R("ie", 0, 2), R("m2", 1, 2), R("cB", 1, 2))
+        act(R("jn", 0, 2), R("ie", 0, 2), 1.0, one("r"))
+        act(R("jn", 2, 4), R("ie", 0, 2), 1.0, one("c6"))
+        act(one("k1"), one("d"), -176.0, 16.0)
+        act(one("k2"), one("d"), -16.0, 320.0)
+        act(one("k3"), one("r2"), -1.0, 4.0, func=F.Relu)
+        act(R("j16"), R("jn"), -1.0, 19.0, func=F.Relu)
+        act(one("k4"), one("d"), 176.0, 128.0)
+        act(one("k6"), one("d"), -352.0, 192.0)
+        act(one("k7"), one("r2"), 1.0, -1.0, func=F.Abs)
+        act(R("ge"), R("j16"), -1.0, 9.5, func=F.Sign)
+        planes("xt", (0,))
+        act(R("ge"), R("ge"), one("k1"), one("k2"))
+        act(one("k4"), one("k3"), -32.0, one("k4"))
         act(one("rof"), one("d"), float(BOTH - FIRST), float(FIRST))
         act(one("rob"), one("d"), float(FIRST - BOTH), float(BOTH))
+        for k in range(4):
+            act(R("base", k, k + 1), R("j16", k, k + 1), -16.0, R("ge", k, k + 1))
+        act(one("kp"), one("b0"), one("k6"), one("k4"))
+        act(one("rs"), one("k7"), -4.0, 4.0, func=F.Relu)
+        planes("xt", (1,))
+        for c0, k, at in ((44, one("rof"), 0), (46, one("rob"), 0), (48, float(ENTRY), 2), (50, float(FIRST), 2), (54, float(BOTH), 2), (56, float(FIRST), 2)):
+            act(R("st", c0, c0 + 2), R("base", at, at + 2), 1.0, k)
+        act(R("st", 52, 53), one("kp"), 1.0, float(FIRST))
+        act(R("st", 53, 54), one("kp"), 1.0, float(MATE))
+        act(one("rz"), one("rs"), -0.5, 2.0)
         act(one("mb"), one("d"), 0.0, 0.5)
+        planes("xt", (2, 3))
         act(one("mb", 3), one("d", 3), 0.0, 0.25)
-        act(one("c6"), one("d"), -32.0, 32.0)
+
+    def inverse(k):
+        src, off = R("bl", 64 * k, 64 * k + 64), R("qo16", 4 * k, 4 * k + 4)
+        return lambda: op("v", [R("sc")], [off, src], lambda: g.vector.tensor_copy(ap(R("sc")).indirect(ap(off)), ap(src)))
+
+    def orders():
+        act(R("rb2", 320, 640), R("sc"), off=R("lb", 32, 52))
+        act(R("rb2", 0, 320), R("sc"), off=R("lb", 0, 20))
+        planes("xt", (4, 5))
 
     first_out = {
-        0: [lambda: turn(R("rt", 0, 640), R("rw", 0, 640))],
-        1: [lambda: table("e2f", 16, "rt", 0, 320), lambda: table("e1f", 0, "rt", 0, 320), lambda: planes("xt")],
-        2: [lambda: lin(R("l2f"), R("ie", 0, 10), 2.0, one("p31"))],
-        3: [lambda: lin(R("pl", 6, 8), R("ie", 0, 2), R("m2", 1, 2), R("cA", 1, 2)), lambda: lin(R("pl", 8, 10), R("ie", 0, 2), R("m2", 1, 2), R("cB", 1, 2))],
-        4: [inverse],
-        5: [orders],
-        6: [lambda: ts(R("jn"), R("ie", 0, 2), one("r"), A.add, 19.0, A.min), lambda: ts(R("l3f"), R("i3"), one("c3"), A.add, 160.0, A.subtract)],
-        7: [lambda: ts(R("ge"), R("jn"), 10.0, A.is_ge, one("cx"), A.mult), lambda: lin(R("j16"), R("jn"), 16.0, one("d160"))],
-        8: [lambda: tt(R("base"), R("ge"), R("j16"), A.add), lambda: ts(one("c4"), one("r2"), 4.0, A.min, 32.0, A.mult)],
-        9: [lambda: ts(R("sef"), R("base"), one("rof"), A.add), lambda: ts(one("c5"), one("cx"), 160.0, A.add, one("b0"), A.mult)],
-        10: [lambda: lin(one("kp"), one("d"), 176.0, one("c4")), lambda: ts(R("al", 0, 2), R("base"), float(FIRST), A.add),
-             lambda: ts(R("al", 2, 4), R("base"), float(ENTRY), A.add)],
-        11: [lambda: ts(R("al", 4, 5), one("kp"), one("c5"), A.add, float(FIRST), A.add), lambda: ts(R("al", 5, 6), one("kp"), one("c5"), A.add, float(MATE), A.add)]}
-    back_lists = [lambda: turn(R("tb2", 320, 640), R("rb2", 320, 640)), lambda: ts(one("rs"), one("r2"), 1.0, A.is_equal, 4.0, A.mult),
-                  lambda: turn(R("tb2", 0, 320), R("rb2", 0, 320)),
-                  lambda: tt(R("km", 0, 20), R("tb2", 320, 640, 16), R("tb2", 321, 640, 16), A.min), lambda: act(one("rz"), one("rs"), -0.5, 2.0),
-                  lambda: table("e1b", 16, "tb2", 0, 1),
-                  lambda: ts(R("krb"), R("km", 1, 20, 2), 160.0, A.add), lambda: ts(R("kb", 0, 10), R("km", 1, 20, 2), 160.0, A.add),
-                  lambda: ts(R("kb", 10, 20), R("km", 0, 20, 2), 160.0, A.add)]
-    unit = [lambda b=b: quant("eq", R("et", 512 * b, 512 * b + 512), 128 * b, 128 * b + 128) for b in (3, 2, 0, 1)]
-    first_back = {0: [lambda: lin(R("l2b"), R("ie", 0, 10), 2.0, one("p31"))], 1: [], 2: [],
-                  3: unit[0:1], 4: [], 5: unit[1:2], 6: unit[2:4],
-                  7: [lambda: ts(R("l3b"), R("i3"), one("c3"), A.add, 160.0, A.subtract), lambda: ts(R("seb"), R("base"), one("rob"), A.add)],
-                  8: [lambda: ts(R("bm", 0, 2), R("base"), float(FIRST), A.add), lambda: ts(R("bm", 2, 4), R("base"), float(BOTH), A.add)],
-                  9: [lambda: fill(R("tw", 0, 1), 0.5), lambda: fill(R("tw", 1, 16), -0.5)]}
+        0: [lambda: turn(R("rt", 0, 640), R("rw", 0, 640)), roles],
+        1: [lambda: tables("e1f", 0, "rt", 0, 320), lambda: tables("e2f", 16, "rt", 0, 320)],
+        2: [lambda: copy(R("sl", 0, 44), R("st", 0, 44))],
+        3: [inverse(0)], 4: [inverse(1)], 5: [inverse(2)], 6: [inverse(3), lambda: ts(R("lb"), R("iw"), 0.0, A.add, off=R("plb"))], 7: [inverse(4), orders],
+        8: [lambda: copy(R("sl", 44, 58), R("st", 44, 58))],
+        10: [lambda: turn(R("tb2", 320, 640), R("rb2", 320, 640))],
+        11: [lambda: tt(R("km", 0, 20), R("tb2", 320, 640, 16), R("tb2", 321, 640, 16), A.min)]}
+    back_lists = [lambda: ts(R("kb", 0, 10), R("km", 1, 20, 2), 160.0, A.add), lambda: ts(R("kb", 10, 20), R("km", 0, 20, 2), 160.0, A.add)]
+    unit = [lambda b=b: quant("eq", R("et", 512 * b, 512 * b + 512), 128 * b, 128 * b + 128) for b in (0, 3, 1, 2)]
+    first_back = {0: unit[0:1], 1: unit[1:2], 2: unit[2:3], 4: unit[3:4], 9: [lambda: table(R("diff"), 16, "rt", 0, 320, A.subtract)], 10: [lambda: table(R("difb"), 0, "tb2", 0, 1, A.subtract)]}
 
+    decide("f")
     for rnd, s in enumerate(ROUNDS):
         peer = T.cores[rank ^ s]
         rid, pid, _se = topo.addr(peer)
         mask, neng = topo.mask(core, peer), len(topo.engines(core, peer))
         last = rnd == 2
-        chain(rnd, "f", first_out if rnd == 0 else {})
+
+        def again():
+            act(R("wr", 0, 320, 1, *quad(3)), R("sgf", 0, 320, 1, *quad(3)))
+        if rnd == 0:
+            chain(rnd, "f", (), first_out)
+            again()
+        else:
+            xo = "xn%d" % (rnd - 1)
+            chain(rnd, "f", (0, 1, 2), {0: [lambda: planes(xo, (0, 1))], 4: [lambda: act(R("r2b"), R("wr"), 2.0, off=R("kb", 10, 20)), lambda: planes(xo, (2,))],
+                                        7: [lambda: planes(xo, (3,)), again] + exchanged("b")[0:1], 8: exchanged("b")[1:2], 10: [lambda: planes(xo, (4, 5))]})
 
         def start1():
             act(R("aa"), R("xf"), off=R("al"))
             tt(R("km3", 0, 10, 1, *quad(3)), R("xf", FIRST, 160, 16, *quad(3)), R("xf", MATE, 160, 16, *quad(3)), A.min)
 
         def start2():
-            lin(R("krb", 0, 10, 1, *quad(3)), R("km3", 0, 10, 1, *quad(3)), 0.5, 800.0)
-            act(R("rb", 0, 160), R("wb"), one("rs"), one("rz"), off=R("krb"))
-            act(R("rb", 160, 320), R("we"), one("rs"), one("rz"), off=R("kb", 10, 20))
+            lin(R("kb", 0, 10, 1, *quad(3)), R("km3", 0, 10, 1, *quad(3)), 0.5, 160.0)
+            act(R("r1b"), R("wr"), one("rs"), one("rz"), off=R("kb", 0, 10))
 
         def start3():
-            lin(R("kb", 0, 10, 1, *quad(3)), R("km3", 0, 10, 1, *quad(3)), 0.5, 160.0)
             tt(R("e1b", 0, 80, 8, *quad(3)), R("aa", 64, 74, 1, *quad(3)), R("aa", 80, 90, 1, *quad(3)), A.subtract)
             tt(R("e1b", 1, 80, 8, *quad(3)), R("aa", 64, 74, 1, *quad(3)), R("aa", 80, 90, 1, *quad(3)), A.add)
-        passes("vt", "xp", "xo", lambda t, c0, c1: R("xi" if t < 2 else "xp", C * t + c0, C * t + c1), (3, 2),
-               {0: [start1], 1: (back_lists if rnd == 0 else []) + [start2]})
+        passes("vt", "xp", "xo", lambda t, c0, c1, fused: R("xi" if fused else "xp", C * t + c0, C * t + c1),
+               ((0, 0, C), (1, 0, 160)), ((3, 0, C), (2, 0, C), (1, 160, C)), {0: (back_lists if rnd == 0 else []) + [start1], 1: [start2], 2: [lambda: turn(R("tb2", 0, 320), R("rb2", 0, 320))] if rnd == 0 else []})
         halves("vq", "vt", True)
+        if rnd == 0:
+            tables("e1b", 16, "tb2", 0, 1)
+            tables("e2b", 0, "tb2", 0, 1)
+        start3()
+        signs("sgb", 0)
+        signs("sgb", 1)
         for h, (c0, c1) in enumerate(HALVES):
             for b in range(4):
+                if (h, b) == (0, DEC):
+                    decide("b")
                 k = ring()
                 mx(k, c1 - c0, "wq", 128 * b, "vq", c0)
                 act(R("ht", 4 * c0 + b, 4 * c1, 4), R("ps%d" % k, 0, c1 - c0), 0.03125)
-        start3()
-        if rnd == 0:
-            table("e2b", 0, "tb2", 0, 1)
-        signs("sgb", 0)
-        signs("sgb", 1)
 
         def send(h):
             c0, c1 = C * rnd + HALVES[h][0], C * rnd + HALVES[h][1]
@@ -451,12 +504,11 @@ def rank_program(g, core, T, topo):
                     mx(k, c1 - c0, "eq", 128 * b, "rq", C * rnd + c0)
                     act(R("dp", C * b + c0, C * b + c1), R("ps%d" % k, 0, c1 - c0))
 
-        gaps = {k: list(v) for k, v in first_back.items()} if rnd == 0 else {}
-        if last:
-            gaps = {5: [lambda: quant("vvq", R("vv"), 0, 128)], 6: [lambda: copy(R("kn"), R("gg", 64, 84)), lambda: ts(R("own"), R("jn"), one("c6"), A.add)]}
-        for k, f in ((1, lambda: send(0)), (4, lambda: send(1)), (7, unpack)):
+        gaps = [{k: list(v) for k, v in first_back.items()}, {},
+                {5: [lambda: quant("vvq", R("vv"), 0, 128)], 6: [lambda: copy(R("kn"), R("gg", 64, 84))]}][rnd]
+        for k, f in ((SEND[0], lambda: send(0)), (SEND[1], lambda: send(1)), (7, unpack)):
             gaps.setdefault(k, []).append(f)
-        chain(rnd, "b", gaps)
+        chain(rnd, "b", SB, gaps)
         xn = "xn%d" % rnd
         cu, old = "cu%d" % (rnd % 2), "cu%d" % (1 - rnd % 2)
 
@@ -468,25 +520,29 @@ def rank_program(g, core, T, topo):
                 tt(R(cu), R(old), R("md"), A.not_equal)
 
         def miss3():
+            for at, k in ((0, EVEN), (32, ODD)):
+                if last:
+                    lin(R("nr", at // 2, 320, 32), R(cu, at, at + 20, 2), -1.0, 0.5)
+                else:
+                    lin(R("nr", k, 320, 16), R(cu, at, at + 20), -1.0, 0.5)
+
+        def miss4():
+            turn(R("wr"), R("nr"))
             if last:
-                ts(R("moff", 0, 32), R(cu), 0.0, A.add, off=R("own"))
-                act(R("wo"), R("tw"), off=R("moff", 0, 20))
-                act(R("q0", 2, 960, 3), R("wo"), -1.0, 0.5, off=R("kn"))
-                return
-            copy(R("moff"), R(cu))
-            for w, at, c0 in (("wo", 0, 160), ("we", 32, 0)):
-                act(R(w), R("tw"), off=R("moff", at, at + 20))
-                act(R("rf", c0, c0 + 160), R(w), one("rs"), one("rz"), off=R("kf", c0 // 16, c0 // 16 + 10))
-        passes(xn, "dp", "xob", lambda t, c0, c1: R("vt", 4 * c0 + t, 4 * c1, 4), (3,), {0: [miss1], 1: [miss2], 2: [miss3]})
+                act(R("q0", 2, 960, 3), R("wr"), -1.0, 0.5, off=R("kn"))
+            else:
+                act(R("r2f"), R("wr"), 2.0, off=R("kf", 10, 20))
+                act(R("r1f"), R("wr"), one("rs"), one("rz"), off=R("kf", 0, 10))
+        passes(xn, "dp", "xob", lambda t, c0, c1, fused: R("vt", 4 * c0 + t, 4 * c1, 4), ((0, 0, C), (1, 0, 160), (1, 160, C)), ((3, 0, C), (2, 0, C)),
+               {0: [miss1], 1: [miss2], 2: [miss3], 3: [miss4]})
         halves("xq", xn, not last)
         if not last:
-            planes(xn)
+            run(maps[rnd])
+            run(exchanged("f")[0:1])
             signs("sgf", 0)
+            run(exchanged("f")[1:2])
             signs("sgf", 1)
-        if rnd == 1:
-            act(R("q1", 0, 960, 3), R("qr"), off=R("mo16"))
-            act(R("q1", 1, 960, 3), R("qr"), -1.0)
-            act(R("q1", 2, 960, 3), R("qr"))
+            decide("f")
 
     dma("y", [], [R("xqc")], T.oc[:, :], T.xqc[:, :].bitcast(dt.uint8))
     for k in range(4):
@@ -495,8 +551,10 @@ def rank_program(g, core, T, topo):
         mx(h, c1 - c0, "vvq", 0, "xq", c0)
         act(R("yt", c0, c1), R("ps%d" % h, 0, c1 - c0))
         dma("y", [], [R("yt", c0, c1)], T.y[:, c0:c1], ap(R("yt", c0, c1)))
-    scan(R("q2"), R("q0"), R("q1"))
-    ts(R("qout"), R("q2", 2, 960, 3), 160.0, A.add)
+    for c0, c1 in HALVES:
+        scan(R("q2", 3 * c0, 3 * c1), R("q0", 3 * c0, 3 * c1), R("q1", 3 * c0, 3 * c1))
+    for c0, c1 in HALVES:
+        ts(R("qout", c0, c1), R("q2", 3 * c0 + 2, 3 * c1, 3), 160.0, A.add)
     dma("s", [], [R("qout")], T.qo[:, :], T.qout[0:128:16, :])
     for sem, val in sorted(pending.items()):
         g.wait_ge(T.sem[sem], val)

from concourse.mybir import dt, AluOpType as A, ActivationFunctionType as F

C = 320
ROUNDS = (1, 2, 4)
HALVES = ((0, 160), (160, 320))
BIG = 1e29
DEC, SEND, SB = 1, (3, 5), (0, 1)

SCRATCH = {}


def _buf(dtype, **widths):
    for k, n in widths.items():
        SCRATCH[k] = ("sbuf", [128, n], dtype)


_buf("bfloat16", xt=1280, xn0=1280, xn1=1280, xn2=1280, xp=1280, xi=640, vt=1280, ht=1280, dp=1280, ut=512, vv=512, et=2048, ones=512,
     iot=320, ys=960, qr=320, rw=1280, rt=1280, bl=320, sc=320, rb2=640, tb2=640, wr=320, nr=320, sgf=320, sgb=320, r1f=160, r1b=160, r2f=160, r2b=160,
     trf=160, trb=160, pk=320, t0=320, m1=80, nn=320, nw=320, g1=160, t2=320, gw=320, zw=480, t3=192, fr=192, xf=352, xb=352,
     aa=96, md=64, cu0=64, cu1=64, km=30, q0=960, q1=960, q2=960)
_buf("float32", col=32, fb=7, sm=48, ie=20, iw=32, i40=40, i23=40, st=58, ef=160, eb=160, dif=20, qout=320, yt=320)
_buf("int32", ib=7, gg=96, iwi=20)
_buf("uint16", offu=8, qo16=20, mo16=20, pl=6, la=96, lb=64, kf=20, kb=20, kn=20, l1=10, sl=60, xo=32, xob=32)
for _n, _w in (("uq", 128), ("us", 128), ("xq", 320), ("vq", 320), ("vvq", 128), ("eq", 512), ("wq", 512), ("hq", 960), ("rq", 960)):
    SCRATCH[_n + "c"] = ("sbuf", [128, _w], "float8_e4m3fn_x4")
    SCRATCH[_n + "s"] = ("sbuf", [128, _w], "uint8")
for _b in range(8):
    SCRATCH["ps%d" % _b] = ("psum", [128, 512], "float32")

NDMA = 20
SEMAPHORES = ["qv", "qs", "qt", "qg", "lsem"] + ["d%d" % i for i in range(NDMA)] + ["ar%d_%d" % (r, h) for r in range(3) for h in range(2)]

PLACE = {n: ("fb", i, 1) for i, n in enumerate(("b0", "b0x", "b1", "r", "r2", "d", "g3"))}
PLACE.update({n: ("col", i, 1) for i, n in enumerate(("thr", "cs", "rs", "rz", "dl", "nd", "xa", "xc", "rd", "p31", "zo", "u16", "rof", "rob", "mb", "fn", "im", "ic",
                                                      "c1", "c2", "c3", "c4", "c5", "c6", "k1", "k2", "k3", "k4", "k6", "k7", "kp"))})
PLACE.update({n: ("sm", 2 * i, 2) for i, n in enumerate(("cS", "cH", "fS", "fH", "tA", "tB", "cA", "cB", "m2"))})
PLACE.update({n: ("sm", 18 + 4 * i, 4) for i, n in enumerate(("jn", "ge", "j16", "base"))})
PLACE.update({n: ("sl", a, w) for n, a, w in (("l2f", 0, 10), ("l2b", 10, 10), ("l3f", 20, 10), ("l3b", 30, 10), ("plb", 40, 4), ("sef", 44, 2), ("seb", 46, 2),
                                              ("al", 48, 6), ("bm", 54, 4))})
PLACE.update({"iu": ("sm", 36, 8), "km3": ("km", 20, 10), "e1f": ("ef", 0, 80), "e2f": ("ef", 80, 80), "e1b": ("eb", 0, 80), "e2b": ("eb", 80, 80),
              "diff": ("dif", 0, 10), "difb": ("dif", 10, 10)})
ENTRY, FIRST, MATE, BOTH = 1, 2, 4, 8
EVEN, ODD = 2, 3


def R(name, c0=0, c1=None, st=1, p0=0, p1=128):
    if name in PLACE:
        name, at, n = PLACE[name]
        return (name, at + c0, at + (n if c1 is None else c1), st, p0, p1)
    return (name, c0, SCRATCH[name][1][1] if c1 is None else c1, st, p0, p1)


def rank_program(g, core, T, topo):
    rank = T.rank_of(core)
    if rank is None:
        return
    queue = {"v": g.vector, "s": g.scalar, "t": g.tensor, "g": g, "y": g.sync}
    count = {"qv": 0, "qs": 0, "qt": 0, "qg": 0}
    known = {k: {} for k in queue}
    clock = {}
    writes, reads = {}, {}
    pending = {}
    state = {"bank": 0, "dma": 0}

    def ap(r):
        name, c0, c1, st, p0, p1 = r
        return T[name][p0:p1, c0:c1:st] if st > 1 else T[name][p0:p1, c0:c1]

    def hit(a, b):
        if a[4] >= b[5] or b[4] >= a[5] or a[1] >= b[2] or b[1] >= a[2]:
            return False
        s = min(a[3], b[3])
        return not (s > 1 and max(a[3], b[3]) % s == 0 and (a[1] - b[1]) % s)

    def inside(a, b):
        return a[4] >= b[4] and a[5] <= b[5] and a[1] >= b[1] and a[2] <= b[2] and (b[3] == 1 or (a[3] == b[3] and (a[1] - b[1]) % a[3] == 0))

    def settle(q, events):
        for sem, val in sorted(events, key=lambda e: (-len(clock[e]), e[0], -e[1])):
            if known[q].get(sem, 0) < val:
                queue[q].wait_ge(T.sem[sem], val)
                for s, v in clock[(sem, val)].items():
                    known[q][s] = max(known[q].get(s, 0), v)
                known[q][sem] = val

    def order(q, outs, ins):
        ev = set()
        for r in ins:
            ev |= {e for w, e in writes.get(r[0], []) if hit(r, w)}
        for r in outs:
            ev |= {e for w, e in writes.get(r[0], []) if hit(r, w)}
            ev |= {e for w, e in reads.get(r[0], []) if hit(r, w)}
        settle(q, ev)

    def note(outs, ins, ev):
        for r in outs:
            for book in (writes, reads):
                book[r[0]] = [(w, e) for w, e in book.get(r[0], []) if not inside(w, r)]
            writes[r[0]].append((r, ev))
        for r in ins:
            reads.setdefault(r[0], []).append((r, ev))

    def op(q, outs, ins, fn):
        order(q, outs, ins)
        sem = "q" + q
        clk = dict(known[q])
        fn().then_inc(T.sem[sem], 1)
        count[sem] += 1
        clk[sem] = count[sem]
        clock[(sem, count[sem])] = clk
        note(outs, ins, (sem, count[sem]))

    def dma(q, outs, ins, dst, src):
        order(q, outs, ins)
        sem = "d%d" % state["dma"]
        state["dma"] += 1
        clock[(sem, 16)] = dict(known[q])
        queue[q].dma_start(dst, src).then_inc(T.sem[sem], 16)
        pending[sem] = 16
        note(outs, ins, (sem, 16))

    def arg(s):
        return ap(s) if isinstance(s, tuple) else s

    def cols(*ss):
        return [s for s in ss if isinstance(s, tuple)]

    def copy(out, src):
        op("v", [out], [src], lambda: g.vector.tensor_copy(ap(out), ap(src)))

    def pick(out, win, off):
        op("v", [out], [win, off], lambda: g.vector.tensor_copy(ap(out), ap(win).indirect(ap(off))))

    def pick_tt(out, win, off, other, alu):
        op("v", [out], [win, off, other], lambda: g.vector.tensor_tensor(ap(out), ap(win).indirect(ap(off)), ap(other), alu))

    def ts(out, src, s1, op0, s2=None, op1=None, off=None):
        def call():
            a = ap(src) if off is None else ap(src).indirect(ap(off))
            if op1 is None:
                return g.vector.tensor_scalar(ap(out), a, arg(s1), None, op0)
            return g.vector.tensor_scalar(ap(out), a, arg(s1), arg(s2), op0, op1)
        op("v", [out], [src] + cols(s1, s2, off), call)

    def lin(out, src, a, b, off=None):
        ts(out, src, a, A.mult, b, A.add, off)

    def tt(out, a, b, alu):
        op("v", [out], [a, b], lambda: g.vector.tensor_tensor(ap(out), ap(a), ap(b), alu))

    def fill(out, val):
        op("v", [out], [], lambda: g.vector.memset(ap(out), val))

    def iota(out, pattern, base, cm=0):
        if SCRATCH[out[0]][2] == "int32":
            op("g", [out], [], lambda: g.iota(ap(out), pattern, base, cm))
        else:
            op("g", [out], [], lambda: g.iota(ap(out), pattern, base, cm, allow_small_or_imprecise_dtypes=True))

    def turn(out, src):
        op("v", [out], [src], lambda: g.vector.transpose(ap(out), ap(src)))

    def scan(out, d0, d1):
        op("v", [out], [d0, d1], lambda: g.vector.tensor_tensor_scan(ap(out), ap(d0), ap(d1), 0.0, A.mult, A.add))

    def quant(name, src, c0, c1):
        o, s = R(name + "c", c0, c1), R(name + "s", c0, c1)
        op("v", [o, s], [src], lambda: g.vector.quantize_mx(ap(o), ap(s), ap(src)))

    def mx(bank, n, wname, w0, mname, m0):
        w, ws, m, ms = R(wname + "c", w0, w0 + 128), R(wname + "s", w0, w0 + 128), R(mname + "c", m0, m0 + n), R(mname + "s", m0, m0 + n)
        o = R("ps%d" % bank, 0, n)
        op("t", [R("ps%d" % bank)], [w, ws, m, ms], lambda: g.tensor.matmul_mx(ap(o), ap(w), ap(ws), ap(m), ap(ms), True, True))

    def act(out, src, scale=1.0, bias=0.0, off=None, func=None):
        func = func or (F.Copy if bias == 0.0 else F.Identity)
        op("s", [out], [src] + cols(scale, bias, off),
           lambda: g.scalar.activation(ap(out), ap(src) if off is None else ap(src).indirect(ap(off)), func, bias=arg(bias), scale=arg(scale)))

    def quad(q):
        return 32 * q, 32 * q + 32

    def one(n, q=None):
        return R(n, 0, 1) if q is None else R(n, 0, 1, 1, *quad(q))

    def run(calls):
        for f in calls:
            f()

    dma("y", [R("gg", 0, 20)], [], ap(R("gg", 0, 20)), T.gq[:, :])
    dma("y", [R("gg", 32, 52)], [], ap(R("gg", 32, 52)), T.gm[:, :])
    dma("y", [R("xt")], [], ap(R("xt")), T.x[:, :])
    dma("s", [R("ut")], [], ap(R("ut")), T.u[:, :])
    order("y", [], [R("xt")])
    dma("y", [R("wqc")], [], T.wqc[:, :].bitcast(dt.uint8), T.wc[:, :])
    dma("y", [R("wqs")], [], T.wqs[:, :], T.ws[:, :])
    dma("y", [R("vv")], [], ap(R("vv")), T.v[:, :])

    iota(R("iwi", 0, 2), [[0, 2]], 0, 1)
    iota(R("ie"), [[16, 20]], 0)
    iota(R("sm", 0, 4), [[-2, 2], [-1, 2]], 2)
    iota(R("iu"), [[32, 4], [0, 2]], -16)
    iota(R("iot"), [[1, C]], -160)
    iota(R("ef"), [[0, 160]], 0)
    iota(R("i40"), [[64, 10], [0, 4]], 0)
    iota(R("nn"), [[0, 320]], 0)
    iota(R("t2"), [[0, 320]], 0)
    iota(R("iw"), [[16, 32]], 0)
    iota(R("i23", 0, 20), [[0, 2], [32, 10]], 0)
    iota(R("i23", 20, 40), [[0, 2], [32, 5], [160, 2]], -160)
    iota(R("bl"), [[1, C]], -160)
    for n in ("t3", "fr"):
        iota(R(n), [[0, 192]], 0)
    iota(R("eb"), [[0, 160]], 0)
    iota(R("ones"), [[0, 512]], 1)
    op("g", [R("wr")], [R("ones")], lambda: g.affine_select(ap(R("wr")), ap(R("ones", 0, 320)), [[0, 320]], A.is_gt, 0.5, 0, 0))
    for b in range(4):
        o = R("et", 512 * b, 512 * b + 512)
        op("g", [o], [R("ones")], lambda o=o, b=b: g.affine_select(ap(o), ap(R("ones")), [[-1, 512]], A.is_equal, 0.0, b, 4))
    iota(R("nr"), [[0, 320]], 0)
    iota(R("q0"), [[0, 320], [1, 3]], 0)

    for c0, c1 in ((20, 32), (52, 64), (84, 96)):
        fill(R("gg", c0, c1), 0)
    for c0, c1, sh, mask in ((0, 2, 0, 1), (2, 3, 1, 1), (3, 4, 0, 15), (4, 5, 1, 7), (5, 6, 4, 1), (6, 7, 4, 3)):
        ts(R("ib", c0, c1), R("iwi", 0, c1 - c0), sh, A.arith_shift_right, mask, A.bitwise_and)
    fill(R("cH", 1, 2), 3.0)
    copy(R("fb"), R("ib"))
    for n, a, b in (("dl", 0, 2), ("nd", 2, 0), ("c1", 2, 4)):
        tt(one(n), R("ib", a, a + 1), R("ib", b, b + 1), A.subtract)
    ts(R("fS", 0, 4), R("cS", 0, 4), one("g3"), A.is_equal)
    ts(one("rd"), one("r"), one("dl"), A.add)
    lin(one("xc"), one("b0"), 8.0, one("c1"))
    lin(one("xa"), one("b1"), 8.0, one("c1"))
    lin(R("tB"), R("fS"), one("nd"), one("rd"))
    lin(R("tA"), R("fS"), one("dl"), one("r"))
    lin(R("m2"), R("fH"), -0.5, 1.0)
    ts(R("iwi"), R("ie"), one("r"), A.add)
    lin(R("cB", 0, 1), R("fH", 0, 1), one("xc"), R("tB", 0, 1))
    lin(R("cA", 0, 1), R("fH", 0, 1), one("xa"), R("tA", 0, 1))
    act(one("u16"), one("b0"), 16.0)
    act(one("thr"), one("r2"), -BIG, BIG)
    act(one("p31"), one("d"), 16.0, one("r"))
    act(one("c4"), one("r2"), func=F.Sign)
    act(one("c5"), one("g3"), 1.0, -1.5, func=F.Sign)
    act(one("zo"), one("d"), -160.0, 320.0)
    act(one("c6"), one("r2"), 2.0, one("d"))
    act(one("fn"), one("p31"), 2.0, -320.0)
    act(one("cs"), one("c4"), 0.5)
    act(one("im"), one("c5"), 0.5, 1.5)
    act(one("c2"), one("c5"), -144.0, 144.0)
    act(one("c3"), one("p31"), 1.0, one("zo"))
    copy(R("qo16"), R("gg", 0, 20))
    lin(R("pl", 2, 4), R("ie", 0, 2), R("m2", 0, 1), R("cB", 0, 1))
    tt(R("gg", 64, 84), R("gg", 32, 52), R("iwi"), A.min)
    lin(R("pl", 0, 2), R("ie", 0, 2), R("m2", 0, 1), R("cA", 0, 1))
    act(R("qr"), R("iot"), off=R("qo16"))
    ts(R("offu"), R("iu"), one("u16"), A.add)
    copy(R("mo16"), R("gg", 32, 52))

    for k, at in ((2, 2), (0, 0), (1, 0)):
        ts(R("la", 32 * k, 32 * k + 32), R("gg", 32 * k, 32 * k + 32), 0.0, A.add, off=R("pl", at, at + 2))
        if k == 2:
            lin(R("offu", 0, 2), R("fb", 0, 2), -112.0, 112.0)
            quant("uq", R("ut"), 0, 128)
    act(R("rw", 640, 960), R("iot"), off=R("la", 64, 84))
    op("s", [R("uss")], [R("uqs"), R("offu")], lambda: g.scalar.activation(T.uss[:, 0:128], T.uqs[:, 0:128].indirect(T.offu[:, 0:8]), F.Copy))
    act(R("rw", 960, 1280), R("iot"), off=R("mo16"))
    act(R("rw", 0, 320), R("iot"), off=R("la", 0, 20))
    op("v", [R("usc")], [R("uqc"), R("offu")], lambda: g.vector.tensor_copy(T.usc[:, 0:128].bitcast(dt.uint32), T.uqc[:, 0:128].bitcast(dt.uint32).indirect(T.offu[:, 0:8])))
    dma("y", [R("bl")], [R("rw", 960, 1280)], T.bl[1:128:2, :], T.rw[1:128:2, 960:1280])

    def signs(name, h):
        c0, c1 = HALVES[h]
        ts(R(name, c0, c1), R("ps%d" % h, 0, c1 - c0), one("thr"), A.is_gt, one("cs"), A.subtract)

    def halves(name, src, decide):
        for h, (c0, c1) in enumerate(HALVES):
            quant(name, R(src, 4 * c0, 4 * c1), c0, c1)
            if decide:
                mx(h, c1 - c0, "us", 0, name, c0)

    def table(out, h, src, no, yes, alu):
        tt(out, R(src, yes + h, yes + 320 - yes % 16, 32), R(src, no + h, no + 320, 32), alu)

    def tables(e, h, src, no, yes):
        table(R(e, 0, 80, 8), h, src, no, yes, A.subtract)
        table(R(e, 1, 80, 8), h, src, no, yes, A.add)

    halves("xq", "xt", True)
    pick(R("rw", 320, 640), R("qr"), R("la", 32, 52))
    turn(R("rt", 640, 960), R("rw", 640, 960))
    signs("sgf", 0)
    ts(R("kf", 0, 10), R("rt", 640, 960, 32), 160.0, A.add)
    ts(R("kf", 10, 20), R("rt", 656, 960, 32), 160.0, A.add)
    act(R("nn", 1, 320, 8), R("i40"), 1.0, one("fn"))
    signs("sgf", 1)
    turn(R("rt", 960, 1280), R("rw", 960, 1280))

    def ring():
        state["bank"] += 1
        return 2 + state["bank"] % 6

    def both(out, at, win, off, share):
        if share:
            act(R(out, at + 96, at + 160), R(win), off=R(off, 6, 10))
            pick(R(out, at, at + 96), R(win), R(off, 0, 6))
        else:
            pick(R(out, at, at + 160), R(win), R(off))

    def decide(d):
        act(R("pk", 160, 320), R("sg" + d), 2.0, off=R("k" + d, 10, 20))

    def chain(rnd, d, share, gaps):
        def gap(k):
            run(gaps.get(k, ()))
        first, hops, src, to = (0, ((0, 1), (2, 3)), 1, (2, 3)) if d == "f" else (1, ((3, 2), (1, 0)), 2, (1, 0))
        if d == "f" and rnd == 0:
            lin(R("pk", 0, 160), R("sgf"), 2.0, 0.0, off=R("kf", 0, 10))
        else:
            pick_tt(R("pk", 0, 160), R("sg" + d), R("k" + d, 0, 10), R("r1" + d), A.mult)
        gap(0)
        for c0, c1 in HALVES:
            turn(R("t0", c0, c1), R("pk", c0, c1))
        gap(1)
        scan(R("m1"), R("t0", first, 160, 2), R("e1" + d))
        scan(R("nn", 0, 320, 4), R("t0", 161 - first, 320, 2), R("e2" + d))
        lin(R("l1"), R("m1", 1, 80, 8), 0.5 if d == "f" else one("mb"), 160.0)
        gap(2)
        turn(R("nw"), R("nn"))
        gap(3)
        both("g1", 0, "nw", "l1", 0 in share)
        gap(4)
        turn(R("t2", 0, 320, 2), R("g1"))
        gap(5)
        turn(R("gw"), R("t2"))
        for a, b in hops:
            lin(R("l2" + d, 0, 10, 1, *quad(b)), R("t2", BOTH, 320, 32, *quad(a)), 0.5, 160.0)
        gap(6)
        both("zw", 160, "gw", "l2" + d, 1 in share)
        gap(7)
        turn(R("t3", 16, 176), R("zw", 160, 320))
        gap(8)
        turn(R("zw", 0, 160), R("t3", 0, 160))
        turn(R("zw", 320, 480), R("t3", 32, 192))
        for b in to:
            lin(R("l3" + d, 0, 10, 1, *quad(b)), R("t3", 16 + BOTH, 176, 16, *quad(src)), 0.5, one("zo", src))
        gap(9)
        both("fr", 16, "zw", "l3" + d, 2 in share)
        gap(10)
        turn(R("x" + d, 0, 160), R("fr", 16, 176))
        turn(R("x" + d, 160, 352), R("fr"))
        gap(11)
        lin(R("xo" if d == "f" else "xob"), R("x" + d), 0.5, 160.0, off=R("se" + d))

    def planes(src, which):
        for k in which:
            t = k % 4
            n = 160 if k == 5 else C
            act(R("xp" if k < 4 else "xi", C * t, C * t + n), R(src, t, 4 * n, 4), 0.5)

    maps = [[lambda: act(R("q1", 0, 960, 3), R("qr"), off=R("mo16"))],
            [lambda: act(R("q1", 1, 960, 3), R("qr"), -1.0), lambda: act(R("q1", 2, 960, 3), R("qr"))]]

    def passes(out, win, off, other, fused, aside, gaps):
        for i, (t, c0, c1) in enumerate(aside):
            act(R("ys", C * i + c0, C * i + c1), R(win, C * t, C * t + C), off=R(off, c0 // 16, c1 // 16))
        run(gaps.get(0, ()))
        for i, (t, c0, c1) in enumerate(fused):
            pick_tt(R(out, 4 * c0 + t, 4 * c1, 4), R(win, C * t, C * t + C), R(off, c0 // 16, c1 // 16), other(t, c0, c1, True), A.add)
            run(gaps.get(1 + i, ()))
        for i, (t, c0, c1) in enumerate(aside):
            for a, b in HALVES if (c1 - c0 == C and i == 1) or len(aside) == 1 else ((c0, c1),):
                tt(R(out, 4 * a + t, 4 * b, 4), R("ys", C * i + a, C * i + b), other(t, a, b, False), A.add)
            run(gaps.get(("add", i), ()))

    def exchanged(d):
        return [lambda: turn(R("tr" + d), R("r2" + d)), lambda: tt(R("e2" + d, 0, 80, 8), R("dif" + d), R("tr" + d, ODD if d == "f" else EVEN, 160, 16), A.mult)]

    def roles():
        for k in range(4):
            act(R("nn", 2 + 8 * k, 320, 32, *quad(3)), R("rt", 976, 1280, 32, *quad(3)), 2.0)
        act(one("ic"), one("d"), one("c2"), one("fn"))
        act(R("iw"), R("iw"), 1.0, one("r"))
        for k in range(2):
            act(R("t2", ENTRY + 16 * k, 320, 32), R("ie", 0, 20, 2), one("im"), one("ic"))
        act(R("cA", 1, 2), R("fH", 1, 2), one("xa"), R("tA", 1, 2))
        act(R("cB", 1, 2), R("fH", 1, 2), one("xc"), R("tB", 1, 2))
        act(R("st", 0, 20), R("i23", 0, 20), 1.0, one("p31"))
        act(R("st", 20, 40), R("i23", 20, 40), 1.0, one("c3"))
        act(R("st", 40, 42), R("ie", 0, 2), R("m2", 1, 2), R("cA", 1, 2))
        act(R("st", 42, 44), R("ie", 0, 2), R("m2", 1, 2), R("cB", 1, 2))
        act(R("jn", 0, 2), R("ie", 0, 2), 1.0, one("r"))
        act(R("jn", 2, 4), R("ie", 0, 2), 1.0, one("c6"))
        act(one("k1"), one("d"), -176.0, 16.0)
        act(one("k2"), one("d"), -16.0, 320.0)
        act(one("k3"), one("r2"), -1.0, 4.0, func=F.Relu)
        act(R("j16"), R("jn"), -1.0, 19.0, func=F.Relu)
        act(one("k4"), one("d"), 176.0, 128.0)
        act(one("k6"), one("d"), -352.0, 192.0)
        act(one("k7"), one("r2"), 1.0, -1.0, func=F.Abs)
        act(R("ge"), R("j16"), -1.0, 9.5, func=F.Sign)
        planes("xt", (0,))
        act(R("ge"), R("ge"), one("k1"), one("k2"))
        act(one("k4"), one("k3"), -32.0, one("k4"))
        act(one("rof"), one("d"), float(BOTH - FIRST), float(FIRST))
        act(one("rob"), one("d"), float(FIRST - BOTH), float(BOTH))
        for k in range(4):
            act(R("base", k, k + 1), R("j16", k, k + 1), -16.0, R("ge", k, k + 1))
        act(one("kp"), one("b0"), one("k6"), one("k4"))
        act(one("rs"), one("k7"), -4.0, 4.0, func=F.Relu)
        planes("xt", (1,))
        for c0, k, at in ((44, one("rof"), 0), (46, one("rob"), 0), (48, float(ENTRY), 2), (50, float(FIRST), 2), (54, float(BOTH), 2), (56, float(FIRST), 2)):
            act(R("st", c0, c0 + 2), R("base", at, at + 2), 1.0, k)
        act(R("st", 52, 53), one("kp"), 1.0, float(FIRST))
        act(R("st", 53, 54), one("kp"), 1.0, float(MATE))
        act(one("rz"), one("rs"), -0.5, 2.0)
        act(one("mb"), one("d"), 0.0, 0.5)
        planes("xt", (2, 3))
        act(one("mb", 3), one("d", 3), 0.0, 0.25)

    def inverse(k):
        src, off = R("bl", 64 * k, 64 * k + 64), R("qo16", 4 * k, 4 * k + 4)
        return lambda: op("v", [R("sc")], [off, src], lambda: g.vector.tensor_copy(ap(R("sc")).indirect(ap(off)), ap(src)))

    def orders():
        act(R("rb2", 320, 640), R("sc"), off=R("lb", 32, 52))
        act(R("rb2", 0, 320), R("sc"), off=R("lb", 0, 20))
        planes("xt", (4, 5))

    first_out = {
        0: [lambda: turn(R("rt", 0, 640), R("rw", 0, 640)), roles],
        1: [lambda: tables("e1f", 0, "rt", 0, 320), lambda: tables("e2f", 16, "rt", 0, 320)],
        2: [lambda: copy(R("sl", 0, 44), R("st", 0, 44))],
        3: [inverse(0)], 4: [inverse(1)], 5: [inverse(2)], 6: [inverse(3), lambda: ts(R("lb"), R("iw"), 0.0, A.add, off=R("plb"))], 7: [inverse(4), orders],
        8: [lambda: copy(R("sl", 44, 58), R("st", 44, 58))],
        10: [lambda: turn(R("tb2", 320, 640), R("rb2", 320, 640))],
        11: [lambda: tt(R("km", 0, 20), R("tb2", 320, 640, 16), R("tb2", 321, 640, 16), A.min)]}
    back_lists = [lambda: ts(R("kb", 0, 10), R("km", 1, 20, 2), 160.0, A.add), lambda: ts(R("kb", 10, 20), R("km", 0, 20, 2), 160.0, A.add)]
    unit = [lambda b=b: quant("eq", R("et", 512 * b, 512 * b + 512), 128 * b, 128 * b + 128) for b in (0, 3, 1, 2)]
    first_back = {0: unit[0:1], 1: unit[1:2], 2: unit[2:3], 4: unit[3:4], 9: [lambda: table(R("diff"), 16, "rt", 0, 320, A.subtract)], 10: [lambda: table(R("difb"), 0, "tb2", 0, 1, A.subtract)]}

    decide("f")
    for rnd, s in enumerate(ROUNDS):
        peer = T.cores[rank ^ s]
        rid, pid, _se = topo.addr(peer)
        mask, neng = topo.mask(core, peer), len(topo.engines(core, peer))
        last = rnd == 2

        def again():
            act(R("wr", 0, 320, 1, *quad(3)), R("sgf", 0, 320, 1, *quad(3)))
        if rnd == 0:
            chain(rnd, "f", (), first_out)
            again()
        else:
            xo = "xn%d" % (rnd - 1)
            chain(rnd, "f", (0, 1, 2), {0: [lambda: planes(xo, (0, 1))], 4: [lambda: act(R("r2b"), R("wr"), 2.0, off=R("kb", 10, 20)), lambda: planes(xo, (2,))],
                                        7: [lambda: planes(xo, (3,)), again] + exchanged("b")[0:1], 8: exchanged("b")[1:2], 10: [lambda: planes(xo, (4, 5))]})

        def start1():
            act(R("aa"), R("xf"), off=R("al"))
            tt(R("km3", 0, 10, 1, *quad(3)), R("xf", FIRST, 160, 16, *quad(3)), R("xf", MATE, 160, 16, *quad(3)), A.min)

        def start2():
            lin(R("kb", 0, 10, 1, *quad(3)), R("km3", 0, 10, 1, *quad(3)), 0.5, 160.0)
            act(R("r1b"), R("wr"), one("rs"), one("rz"), off=R("kb", 0, 10))

        def start3():
            tt(R("e1b", 0, 80, 8, *quad(3)), R("aa", 64, 74, 1, *quad(3)), R("aa", 80, 90, 1, *quad(3)), A.subtract)
            tt(R("e1b", 1, 80, 8, *quad(3)), R("aa", 64, 74, 1, *quad(3)), R("aa", 80, 90, 1, *quad(3)), A.add)
        passes("vt", "xp", "xo", lambda t, c0, c1, fused: R("xi" if fused else "xp", C * t + c0, C * t + c1),
               ((0, 0, C), (1, 0, 160)), ((3, 0, C), (2, 0, C), (1, 160, C)), {0: (back_lists if rnd == 0 else []) + [start1], 1: [start2], 2: [lambda: turn(R("tb2", 0, 320), R("rb2", 0, 320))] if rnd == 0 else []})
        halves("vq", "vt", True)
        if rnd == 0:
            tables("e1b", 16, "tb2", 0, 1)
            tables("e2b", 0, "tb2", 0, 1)
        start3()
        signs("sgb", 0)
        signs("sgb", 1)
        for h, (c0, c1) in enumerate(HALVES):
            for b in range(4):
                if (h, b) == (0, DEC):
                    decide("b")
                k = ring()
                mx(k, c1 - c0, "wq", 128 * b, "vq", c0)
                act(R("ht", 4 * c0 + b, 4 * c1, 4), R("ps%d" % k, 0, c1 - c0), 0.03125)

        def send(h):
            c0, c1 = C * rnd + HALVES[h][0], C * rnd + HALVES[h][1]
            quant("hq", R("ht", 4 * HALVES[h][0], 4 * HALVES[h][1]), c0, c1)
            order("g", [], [R("hqc", c0, c1), R("hqs", c0, c1)])
            sem = "ar%d_%d" % (rnd, h)
            g.remote_dma(T.rqc[:, c0:c1].bitcast(dt.uint8), T.hqc[:, c0:c1].bitcast(dt.uint8), T.sem[sem], T.sem.lsem, pid, rid, mask)
            g.remote_dma(T.rqs[:, c0:c1], T.hqs[:, c0:c1], T.sem[sem], T.sem.lsem, pid, rid, mask)
            pending["lsem"] = pending.get("lsem", 0) + 2 * neng
            pending[sem] = 2 * neng
            clock[(sem, 2 * neng)] = {}
            note([R("rqc", c0, c1), R("rqs", c0, c1)], [], (sem, 2 * neng))

        def unpack():
            for h, (c0, c1) in enumerate(HALVES):
                for b in (0, 3, 1, 2):
                    k = ring()
                    mx(k, c1 - c0, "eq", 128 * b, "rq", C * rnd + c0)
                    act(R("dp", C * b + c0, C * b + c1), R("ps%d" % k, 0, c1 - c0))

        gaps = [{k: list(v) for k, v in first_back.items()}, {},
                {5: [lambda: quant("vvq", R("vv"), 0, 128)], 6: [lambda: copy(R("kn"), R("gg", 64, 84))]}][rnd]
        for k, f in ((SEND[0], lambda: send(0)), (SEND[1], lambda: send(1)), (7, unpack)):
            gaps.setdefault(k, []).append(f)
        chain(rnd, "b", SB, gaps)
        xn = "xn%d" % rnd
        cu, old = "cu%d" % (rnd % 2), "cu%d" % (1 - rnd % 2)

        def miss1():
            pick_tt(R("md" if rnd else cu), R("xb"), R("bm"), R("aa", 0, 64), A.not_equal)

        def miss2():
            if rnd:
                tt(R(cu), R(old), R("md"), A.not_equal)

        def miss3():
            for at, k in ((0, EVEN), (32, ODD)):
                if last:
                    lin(R("nr", at // 2, 320, 32), R(cu, at, at + 20, 2), -1.0, 0.5)
                else:
                    lin(R("nr", k, 320, 16), R(cu, at, at + 20), -1.0, 0.5)

        def miss4():
            turn(R("wr"), R("nr"))
            if last:
                act(R("q0", 2, 960, 3), R("wr"), -1.0, 0.5, off=R("kn"))
            else:
                act(R("r2f"), R("wr"), 2.0, off=R("kf", 10, 20))
                act(R("r1f"), R("wr"), one("rs"), one("rz"), off=R("kf", 0, 10))
        passes(xn, "dp", "xob", lambda t, c0, c1, fused: R("vt", 4 * c0 + t, 4 * c1, 4), ((0, 0, C), (1, 0, 160), (1, 160, C)), ((3, 0, C), (2, 0, C)),
               {0: [miss1], 1: [miss2], 2: [miss3], 3: [miss4]})
        halves("xq", xn, not last)
        if not last:
            run(maps[rnd])
            run(exchanged("f")[0:1])
            signs("sgf", 0)
            run(exchanged("f")[1:2])
            signs("sgf", 1)
            decide("f")

    dma("y", [], [R("xqc")], T.oc[:, :], T.xqc[:, :].bitcast(dt.uint8))
    for k in range(4):
        dma("y", [], [R("xqs")], T.osc[4 * k:4 * k + 4, :], T.xqs[32 * k:32 * k + 4, :])
    for h, (c0, c1) in enumerate(HALVES):
        mx(h, c1 - c0, "vvq", 0, "xq", c0)
        act(R("yt", c0, c1), R("ps%d" % h, 0, c1 - c0))
        dma("y", [], [R("yt", c0, c1)], T.y[:, c0:c1], ap(R("yt", c0, c1)))
    for c0, c1 in HALVES:
        scan(R("q2", 3 * c0, 3 * c1), R("q0", 3 * c0, 3 * c1), R("q1", 3 * c0, 3 * c1))
    for c0, c1 in HALVES:
        ts(R("qout", c0, c1), R("q2", 3 * c0 + 2, 3 * c1, 3), 160.0, A.add)
    dma("s", [], [R("qout")], T.qo[:, :], T.qout[0:128:16, :])
    for sem, val in sorted(pending.items()):
        g.wait_ge(T.sem[sem], val)
    for sem, val in count.items():
        g.wait_ge(T.sem[sem], val)
